import numpy as np
import ml_dtypes


def mxq(x, axis, fmt="e4m3"):
    dtype, down = {"e4m3": (ml_dtypes.float8_e4m3fn, 7), "e5m2": (ml_dtypes.float8_e5m2, 14)}[fmt]
    v = np.moveaxis(np.asarray(x, np.float32).astype(ml_dtypes.bfloat16).astype(np.float64), axis, -1)
    blocks = v.reshape(v.shape[:-1] + (-1, 32))
    amax = np.abs(blocks).max(-1, keepdims=True)
    byte = np.maximum(np.where(amax > 0, np.frexp(amax)[1] - 1 + 127, 0) - down, 1)
    scale = np.exp2(byte - 127.0)
    codes = (blocks / scale).astype(np.float32).astype(dtype).astype(np.float64)
    return np.moveaxis((codes * scale).reshape(v.shape), -1, axis)


WIDE = False


def mx_kscale(k):
    if not WIDE:
        return np.ones(k)
    levels = np.array([10, -10, 5, -5, 0])
    if k % 512:
        return np.exp2(np.random.permutation(np.resize(levels, k // 32))).repeat(32)
    a = np.empty((k // 512, 16))
    for p in range(k // 512):
        a[p, :8] = np.random.permutation(np.resize(levels, 8))
        for g in range(8):
            far = levels[np.abs(levels - a[p, g]) >= 10]
            a[p, g + 8] = far[np.random.randint(len(far))]
    return np.exp2(a.ravel()).repeat(32)


def f64(x):
    return np.asarray(x).astype(np.float64)


def striped(idx):
    return np.tile(idx.reshape(-1, 16).T, (8, 1)).astype(np.uint16)


def unstriped(offs):
    return offs[:16].T.reshape(-1).astype(np.int64)


def striped8(idx):
    return np.concatenate([x.reshape(-1, 16).T for x in idx]).astype(np.uint16)


def runs(offs, k):
    lists = np.stack([offs[16 * r : 16 * r + 16].T.reshape(-1) for r in range(8)]).astype(np.int64)
    return lists[np.arange(k) % 512 // 64]


def pack_weight(w):
    k, n = w.shape
    w = f64(np.asarray(w, np.float32).astype(ml_dtypes.bfloat16)).reshape(k // 32, 32, n)
    amax = np.abs(w).max(1)
    byte = np.clip(np.where(amax > 0, np.frexp(amax)[1] - 1 + 127 - 7, 1), 1, 254)
    scaled = (w * np.exp2(127.0 - byte)[:, None, :]).reshape(k, n).astype(np.float32)
    words = np.ascontiguousarray(scaled.reshape(k // 512, 128, 4, n).transpose(0, 1, 3, 2)).astype(ml_dtypes.float8_e4m3fn).view(np.uint8)
    return words, np.ascontiguousarray(byte.astype(np.uint8).reshape(k // 512, 16, n))


def unpack_weight(words, scales):
    g, p, n, _ = words.shape
    vals = np.ascontiguousarray(words).view(ml_dtypes.float8_e4m3fn).astype(np.float64) * np.repeat(np.exp2(scales.astype(np.float64) - 127.0), 8, axis=1)[..., None]
    return vals.transpose(0, 1, 3, 2).reshape(g * 512, n)

def planes(y):
    n, m = y.shape
    v = y.astype(np.float32).astype(ml_dtypes.bfloat16).astype(np.float64).reshape(n // 32, 32, m)
    top = np.abs(v).max(1)
    byte = np.clip(np.where(top > 0, np.frexp(top)[1] - 1 + 127 - 7, 1), 1, 254)
    codes = (v * np.exp2(127.0 - byte)[:, None, :]).reshape(n, m).astype(np.float32).astype(ml_dtypes.float8_e4m3fn).view(np.uint8)
    words = codes.reshape(n // 512, 128, 4, m).transpose(0, 1, 3, 2)
    return np.ascontiguousarray(words), np.ascontiguousarray(byte.astype(np.uint8).reshape(n // 512, 16, m))


K, T, S, N = 512, 2048, 512, 512


def setup_inputs():
    n = np.random.standard_normal
    s = mx_kscale(K)[:, None]
    packed_xT = pack_weight(n((K, T)) * s)
    return {
        "x_words": packed_xT[0],
        "x_scales": packed_xT[1],
        "w1": (n((K, N)) / np.sqrt(K) / s).astype(np.float32),
        "rw": n((N, S)).astype(np.float32),
        "offs": striped(np.random.permutation(T)[:S]),
        "nx": striped8(np.stack([np.random.permutation(S) for _ in range(8)])),
    }


def reference(x_words, x_scales, w1, rw, offs, nx):
    xq = unpack_weight(x_words, x_scales)[:, unstriped(offs)]
    y = mxq(f64(w1), 0, "e4m3").T @ xq
    d = f64(rw) + 0.9 * (y[np.arange(N)[:, None], runs(nx, N)]) - y
    d2 = d + 0.75 * (d[np.arange(N)[:, None], runs(nx, N)])
    out_0 = d + 0.75 * (d2[np.arange(N)[:, None], runs(nx, N)])
    return (out_0,) + planes(out_0)

@@ -1,0 +1,139 @@
+from contextlib import ExitStack
+
+import concourse.mybir as mybir
+
+K, T, S, N = 512, 2048, 512, 512
+FLOPS = 2 * K * N * S
+
+F32 = mybir.dt.float32
+BF16 = mybir.dt.bfloat16
+I32 = mybir.dt.int32
+U32 = mybir.dt.uint32
+U16 = mybir.dt.uint16
+U8 = mybir.dt.uint8
+FP8X4 = mybir.dt.float8_e4m3fn_x4
+COPY = mybir.ActivationFunctionType.Copy
+ADD = mybir.AluOpType.add
+SUBTRACT = mybir.AluOpType.subtract
+
+P = 128
+PACK = 4
+LIST_ROWS = 16
+HALF = S // 2
+GAMMA = 0.9
+DAMP = 0.75
+CHUNKS = ((0, 256), (256, 384), (384, 512))
+
+
+def tile_picked_gae8_none_po_kernel(
+    tc, x_words, x_scales, w1, rw, offs, nx, out_0, out_1, out_2
+):
+    nc = tc.nc
+    with ExitStack() as ctx:
+        lists = ctx.enter_context(tc.tile_pool(name="lists", bufs=1))
+        keep = ctx.enter_context(tc.tile_pool(name="keep", bufs=1))
+        psum = ctx.enter_context(tc.psum_pool(name="psum", bufs=1))
+
+        offs_sb = lists.tile([P, S // LIST_ROWS], U16, name="offs_sb")
+        nx_sb = lists.tile([P, S // LIST_ROWS], U16, name="nx_sb")
+        w_raw = keep.tile([P, PACK, N], F32, name="w_raw")
+        words = keep.tile([P, T], I32, name="words")
+        scales = keep.tile([P, T], U8, name="scales")
+        win_y = [keep.tile([P, 2 * S], F32, name=f"win_y{t}") for t in range(PACK)]
+
+        nc.vector.memset(scales[:].bitcast(I32), 0)
+        nc.sync.dma_start(offs_sb[:], offs)
+        nc.sync.dma_start(nx_sb[:], nx)
+        nc.sync.dma_start(w_raw[:], w1.rearrange("(p j) c -> p j c", j=PACK))
+        for q in range(4):
+            nc.scalar.dma_start(
+                scales[32 * q : 32 * q + 4, :].bitcast(I32), x_scales[0, 4 * q : 4 * q + 4, :].bitcast(I32)
+            )
+        nc.sync.dma_start(words[:], x_words[0].rearrange("p n t -> p (n t)").bitcast(I32))
+        rw_rows = rw.rearrange("(p t) c -> p t c", t=PACK)
+        rw_sb = [keep.tile([P, 2, S], F32, name=f"rw_sb{u}") for u in range(2)]
+        for u in range(2):
+            nc.sync.dma_start(rw_sb[u][:], rw_rows[:, 2 * u : 2 * u + 2, :])
+
+        x_sc = keep.tile([P, S], U8, name="x_sc", align_bytes=64)
+        nc.vector.tensor_copy(x_sc[:], scales[:].indirect(offs_sb[:]))
+
+        w_codes = []
+        w_sc = []
+        w_in = w_raw[:].rearrange("p j (m t) -> p m j t", t=PACK)
+        w_bf = [keep.tile([P, 2 * P * PACK], BF16, name=f"w_bf{u}", align_bytes=64) for u in range(2)]
+        w_out = [w_bf[u][:].rearrange("p (t m j) -> p m j t", t=2, j=PACK) for u in range(2)]
+        nc.vector.tensor_copy(w_out[0], w_in[:, :, :, 0:2])
+        nc.scalar.activation(w_out[1], w_in[:, :, :, 2:4], COPY)
+        for u in range(2):
+            codes = keep.tile([P, 2 * P], U32, name=f"w_codes{u}", align_bytes=64)
+            plane = keep.tile([P, 2 * P], U8, name=f"w_sc{u}", align_bytes=64)
+            nc.vector.quantize_mx(out=codes[:].bitcast(FP8X4), scales=plane[:], in_=w_bf[u][:])
+            for s in range(2):
+                w_codes.append(codes[:, s * P : (s + 1) * P])
+                w_sc.append(plane[:, s * P : (s + 1) * P])
+
+        x_codes = []
+        for h in range(2):
+            picked = keep.tile([P, HALF], U32, name=f"x_codes{h}", align_bytes=64)
+            cols = slice(h * HALF // LIST_ROWS, (h + 1) * HALF // LIST_ROWS)
+            nc.vector.tensor_copy(picked[:], words[:].bitcast(U32).indirect(offs_sb[:, cols]))
+            x_codes.append(picked)
+
+        err = [win_y[(t - 1) % PACK][:, S:] for t in range(PACK)]
+        for u, h in ((0, 0), (0, 1), (1, 0), (1, 1)):
+            cols = slice(h * HALF, (h + 1) * HALF)
+            for t in (2 * u, 2 * u + 1):
+                y = psum.tile([P, HALF], F32, name=f"y{t}{h}")
+                nc.tensor.matmul_mx(
+                    out=y[:],
+                    lhsT=w_codes[t].bitcast(FP8X4),
+                    lhsT_scale=w_sc[t],
+                    rhs=x_codes[h][:].bitcast(FP8X4),
+                    rhs_scale=x_sc[:, cols],
+                    start=True,
+                    stop=True,
+                )
+                nc.vector.tensor_tensor(err[t][:, cols], rw_sb[u][:, t % 2, cols], y[:], SUBTRACT)
+                nc.scalar.activation(win_y[t][:, cols], y[:], COPY, scale=GAMMA)
+
+        win_d = [keep.tile([P, 2 * S], F32, name=f"win_d{t}") for t in range(PACK)]
+        d_damped = [keep.tile([P, S], F32, name=f"d_damped{t}") for t in range(PACK)]
+        for t in range(PACK):
+            nc.vector.tensor_tensor(win_d[t][:, S:], win_y[t][:].indirect(nx_sb[:]), err[t], ADD)
+            nc.scalar.activation(win_d[t][:, :S], win_d[t][:, S:], COPY, scale=DAMP * DAMP)
+            nc.scalar.activation(d_damped[t][:], win_d[t][:, S:], COPY, scale=DAMP)
+
+        win_d2 = [keep.tile([P, S], F32, name=f"win_d2{t}") for t in range(PACK)]
+        for t in range(PACK):
+            nc.vector.tensor_tensor(win_d2[t][:], win_d[t][:].indirect(nx_sb[:]), d_damped[t][:], ADD)
+
+        out_rows = out_0.rearrange("(p t) c -> p t c", t=PACK)
+        out_words = out_1[0].rearrange("p n t -> p (n t)").bitcast(I32)
+        o_sc = keep.tile([P, S], U8, name="o_sc", align_bytes=64)
+        for c, (c0, c1) in enumerate(CHUNKS):
+            width = c1 - c0
+            res = keep.tile([P, PACK, width], F32, name=f"res{c}")
+            for t in range(PACK):
+                nc.vector.tensor_tensor(
+                    res[:, t, :],
+                    win_d2[t][:].indirect(nx_sb[:, c0 // LIST_ROWS : c1 // LIST_ROWS]),
+                    win_d[t][:, S + c0 : S + c1],
+                    ADD,
+                )
+            nc.sync.dma_start(out_rows[:, :, c0:c1], res[:])
+            res_bf = keep.tile([P, width * PACK], BF16, name=f"res_bf{c}", align_bytes=64)
+            dst = res_bf[:].rearrange("p (c i t) -> p c t i", i=4, t=PACK)
+            src = res[:].rearrange("p t (c i) -> p c t i", i=4)
+            if c < len(CHUNKS) - 1:
+                nc.scalar.copy(dst, src)
+            else:
+                nc.vector.tensor_copy(dst, src)
+            o_codes = keep.tile([P, width], I32, name=f"o_codes{c}", align_bytes=64)
+            nc.vector.quantize_mx(out=o_codes[:].bitcast(FP8X4), scales=o_sc[:, c0:c1], in_=res_bf[:])
+            nc.sync.dma_start(out_words[:, c0:c1], o_codes[:])
+        for q in range(4):
+            queue = nc.scalar if q % 2 == 0 else nc.sync
+            queue.dma_start(
+                out_2[0, 4 * q : 4 * q + 4, :].bitcast(I32), o_sc[32 * q : 32 * q + 4, :].bitcast(I32)
+            )

@@ -22,7 +22,7 @@ LIST_ROWS = 16
 HALF = S // 2
 GAMMA = 0.9
 DAMP = 0.75
-CHUNKS = ((0, 256), (256, 384), (384, 512))
+CHUNK = 128
 
 
 def tile_picked_gae8_none_po_kernel(
@@ -36,7 +36,7 @@ def tile_picked_gae8_none_po_kernel(
 
         offs_sb = lists.tile([P, S // LIST_ROWS], U16, name="offs_sb")
         nx_sb = lists.tile([P, S // LIST_ROWS], U16, name="nx_sb")
-        w_raw = keep.tile([P, PACK, N], F32, name="w_raw")
+        w_raw = [keep.tile([P, PACK, N // 2], F32, name=f"w_raw{h}") for h in range(2)]
         words = keep.tile([P, T], I32, name="words")
         scales = keep.tile([P, T], U8, name="scales")
         win_y = [keep.tile([P, 2 * S], F32, name=f"win_y{t}") for t in range(PACK)]
@@ -44,41 +44,38 @@ def tile_picked_gae8_none_po_kernel(
         nc.vector.memset(scales[:].bitcast(I32), 0)
         nc.sync.dma_start(offs_sb[:], offs)
         nc.sync.dma_start(nx_sb[:], nx)
-        nc.sync.dma_start(w_raw[:], w1.rearrange("(p j) c -> p j c", j=PACK))
+        w_rows = w1.rearrange("(p j) c -> p j c", j=PACK)
+        nc.sync.dma_start(w_raw[0][:], w_rows[:, :, : N // 2])
         for q in range(4):
-            nc.scalar.dma_start(
+            nc.sync.dma_start(
                 scales[32 * q : 32 * q + 4, :].bitcast(I32), x_scales[0, 4 * q : 4 * q + 4, :].bitcast(I32)
             )
+        nc.sync.dma_start(w_raw[1][:], w_rows[:, :, N // 2 :])
         nc.sync.dma_start(words[:], x_words[0].rearrange("p n t -> p (n t)").bitcast(I32))
         rw_rows = rw.rearrange("(p t) c -> p t c", t=PACK)
         rw_sb = [keep.tile([P, 2, S], F32, name=f"rw_sb{u}") for u in range(2)]
         for u in range(2):
             nc.sync.dma_start(rw_sb[u][:], rw_rows[:, 2 * u : 2 * u + 2, :])
 
+        w_bf = keep.tile([P, N * PACK], BF16, name="w_bf", tag="operand", align_bytes=64)
+        w_out = w_bf[:].rearrange("p (t m j) -> p m j t", t=PACK, j=PACK)
+        w_in = [w_raw[h][:].rearrange("p j (m t) -> p m j t", t=PACK) for h in range(2)]
+        nc.vector.tensor_copy(w_out[:, : P // 2], w_in[0])
+        nc.scalar.activation(w_out[:, P // 2 :], w_in[1], COPY)
+
         x_sc = keep.tile([P, S], U8, name="x_sc", align_bytes=64)
         nc.vector.tensor_copy(x_sc[:], scales[:].indirect(offs_sb[:]))
 
-        w_codes = []
-        w_sc = []
-        w_in = w_raw[:].rearrange("p j (m t) -> p m j t", t=PACK)
-        w_bf = [keep.tile([P, 2 * P * PACK], BF16, name=f"w_bf{u}", align_bytes=64) for u in range(2)]
-        w_out = [w_bf[u][:].rearrange("p (t m j) -> p m j t", t=2, j=PACK) for u in range(2)]
-        nc.vector.tensor_copy(w_out[0], w_in[:, :, :, 0:2])
-        nc.scalar.activation(w_out[1], w_in[:, :, :, 2:4], COPY)
-        for u in range(2):
-            codes = keep.tile([P, 2 * P], U32, name=f"w_codes{u}", align_bytes=64)
-            plane = keep.tile([P, 2 * P], U8, name=f"w_sc{u}", align_bytes=64)
-            nc.vector.quantize_mx(out=codes[:].bitcast(FP8X4), scales=plane[:], in_=w_bf[u][:])
-            for s in range(2):
-                w_codes.append(codes[:, s * P : (s + 1) * P])
-                w_sc.append(plane[:, s * P : (s + 1) * P])
+        w_codes = keep.tile([P, N], U32, name="w_codes", align_bytes=64)
+        w_sc = keep.tile([P, N], U8, name="w_sc", align_bytes=64)
+        nc.vector.quantize_mx(out=w_codes[:].bitcast(FP8X4), scales=w_sc[:], in_=w_bf[:])
 
-        x_codes = []
+        x_codes = keep.tile([P, S], U32, name="x_codes", tag="operand", align_bytes=64)
         for h in range(2):
-            picked = keep.tile([P, HALF], U32, name=f"x_codes{h}", align_bytes=64)
             cols = slice(h * HALF // LIST_ROWS, (h + 1) * HALF // LIST_ROWS)
-            nc.vector.tensor_copy(picked[:], words[:].bitcast(U32).indirect(offs_sb[:, cols]))
-            x_codes.append(picked)
+            nc.vector.tensor_copy(
+                x_codes[:, h * HALF : (h + 1) * HALF], words[:].bitcast(U32).indirect(offs_sb[:, cols])
+            )
 
         err = [win_y[(t - 1) % PACK][:, S:] for t in range(PACK)]
         for u, h in ((0, 0), (0, 1), (1, 0), (1, 1)):
@@ -87,9 +84,9 @@ def tile_picked_gae8_none_po_kernel(
                 y = psum.tile([P, HALF], F32, name=f"y{t}{h}")
                 nc.tensor.matmul_mx(
                     out=y[:],
-                    lhsT=w_codes[t].bitcast(FP8X4),
-                    lhsT_scale=w_sc[t],
-                    rhs=x_codes[h][:].bitcast(FP8X4),
+                    lhsT=w_codes[:, t * P : (t + 1) * P].bitcast(FP8X4),
+                    lhsT_scale=w_sc[:, t * P : (t + 1) * P],
+                    rhs=x_codes[:, cols].bitcast(FP8X4),
                     rhs_scale=x_sc[:, cols],
                     start=True,
                     stop=True,
@@ -98,7 +95,7 @@ def tile_picked_gae8_none_po_kernel(
                 nc.scalar.activation(win_y[t][:, cols], y[:], COPY, scale=GAMMA)
 
         win_d = [keep.tile([P, 2 * S], F32, name=f"win_d{t}") for t in range(PACK)]
-        d_damped = [keep.tile([P, S], F32, name=f"d_damped{t}") for t in range(PACK)]
+        d_damped = [keep.tile([P, S], F32, name=f"d_damped{t}", tag=f"slot{t}", align_bytes=64) for t in range(PACK)]
         for t in range(PACK):
             nc.vector.tensor_tensor(win_d[t][:, S:], win_y[t][:].indirect(nx_sb[:]), err[t], ADD)
             nc.scalar.activation(win_d[t][:, :S], win_d[t][:, S:], COPY, scale=DAMP * DAMP)
@@ -111,9 +108,14 @@ def tile_picked_gae8_none_po_kernel(
         out_rows = out_0.rearrange("(p t) c -> p t c", t=PACK)
         out_words = out_1[0].rearrange("p n t -> p (n t)").bitcast(I32)
         o_sc = keep.tile([P, S], U8, name="o_sc", align_bytes=64)
-        for c, (c0, c1) in enumerate(CHUNKS):
-            width = c1 - c0
-            res = keep.tile([P, PACK, width], F32, name=f"res{c}")
+        first = keep.tile([P, PACK, 2 * CHUNK], F32, name="res01", tag="slot3", align_bytes=64)
+        for c in range(S // CHUNK):
+            c0, c1 = c * CHUNK, (c + 1) * CHUNK
+            if c < 2:
+                res = first[:, :, c0:c1]
+            else:
+                later = keep.tile([P, PACK, CHUNK], F32, name=f"res{c}", tag=f"bf{c - 2}", align_bytes=64)
+                res = later[:]
             for t in range(PACK):
                 nc.vector.tensor_tensor(
                     res[:, t, :],
@@ -121,15 +123,18 @@ def tile_picked_gae8_none_po_kernel(
                     win_d[t][:, S + c0 : S + c1],
                     ADD,
                 )
-            nc.sync.dma_start(out_rows[:, :, c0:c1], res[:])
-            res_bf = keep.tile([P, width * PACK], BF16, name=f"res_bf{c}", align_bytes=64)
+            if c == 1:
+                nc.sync.dma_start(out_rows[:, :, :c1], first[:])
+            elif c > 1:
+                nc.sync.dma_start(out_rows[:, :, c0:c1], res)
+            res_bf = keep.tile([P, CHUNK * PACK], BF16, name=f"res_bf{c}", tag=f"bf{c}", align_bytes=64)
             dst = res_bf[:].rearrange("p (c i t) -> p c t i", i=4, t=PACK)
-            src = res[:].rearrange("p t (c i) -> p c t i", i=4)
-            if c < len(CHUNKS) - 1:
+            src = res.rearrange("p t (c i) -> p c t i", i=4)
+            if c < S // CHUNK - 1:
                 nc.scalar.copy(dst, src)
             else:
                 nc.vector.tensor_copy(dst, src)
-            o_codes = keep.tile([P, width], I32, name=f"o_codes{c}", align_bytes=64)
+            o_codes = keep.tile([P, CHUNK], I32, name=f"o_codes{c}", align_bytes=64)
             nc.vector.quantize_mx(out=o_codes[:].bitcast(FP8X4), scales=o_sc[:, c0:c1], in_=res_bf[:])
             nc.sync.dma_start(out_words[:, c0:c1], o_codes[:])
         for q in range(4):

@@ -23,6 +23,7 @@ HALF = S // 2
 GAMMA = 0.9
 DAMP = 0.75
 CHUNK = 128
+CAST_SPLIT = 32
 
 
 def tile_picked_gae8_none_po_kernel(
@@ -36,32 +37,33 @@ def tile_picked_gae8_none_po_kernel(
 
         offs_sb = lists.tile([P, S // LIST_ROWS], U16, name="offs_sb")
         nx_sb = lists.tile([P, S // LIST_ROWS], U16, name="nx_sb")
-        w_raw = [keep.tile([P, PACK, N // 2], F32, name=f"w_raw{h}") for h in range(2)]
+        w_raw = [keep.tile([P, 2, N], F32, name=f"w_raw{h}") for h in range(2)]
         words = keep.tile([P, T], I32, name="words")
         scales = keep.tile([P, T], U8, name="scales")
         win_y = [keep.tile([P, 2 * S], F32, name=f"win_y{t}") for t in range(PACK)]
 
         nc.vector.memset(scales[:].bitcast(I32), 0)
         nc.sync.dma_start(offs_sb[:], offs)
-        nc.sync.dma_start(nx_sb[:], nx)
         w_rows = w1.rearrange("(p j) c -> p j c", j=PACK)
-        nc.sync.dma_start(w_raw[0][:], w_rows[:, :, : N // 2])
+        nc.sync.dma_start(w_raw[0][:], w_rows[:, 0:2, :])
+        nc.sync.dma_start(nx_sb[:], nx)
+        nc.sync.dma_start(w_raw[1][:], w_rows[:, 2:4, :])
         for q in range(4):
             nc.sync.dma_start(
                 scales[32 * q : 32 * q + 4, :].bitcast(I32), x_scales[0, 4 * q : 4 * q + 4, :].bitcast(I32)
             )
-        nc.sync.dma_start(w_raw[1][:], w_rows[:, :, N // 2 :])
         nc.sync.dma_start(words[:], x_words[0].rearrange("p n t -> p (n t)").bitcast(I32))
         rw_rows = rw.rearrange("(p t) c -> p t c", t=PACK)
-        rw_sb = [keep.tile([P, 2, S], F32, name=f"rw_sb{u}") for u in range(2)]
-        for u in range(2):
-            nc.sync.dma_start(rw_sb[u][:], rw_rows[:, 2 * u : 2 * u + 2, :])
+        rw_sb = [keep.tile([P, S], F32, name=f"rw_sb{t}") for t in range(PACK)]
+        for t in range(PACK):
+            nc.sync.dma_start(rw_sb[t][:], rw_rows[:, t, :])
 
         w_bf = keep.tile([P, N * PACK], BF16, name="w_bf", tag="operand", align_bytes=64)
         w_out = w_bf[:].rearrange("p (t m j) -> p m j t", t=PACK, j=PACK)
         w_in = [w_raw[h][:].rearrange("p j (m t) -> p m j t", t=PACK) for h in range(2)]
-        nc.vector.tensor_copy(w_out[:, : P // 2], w_in[0])
-        nc.scalar.activation(w_out[:, P // 2 :], w_in[1], COPY)
+        nc.vector.tensor_copy(w_out[:, :, 0:2, :], w_in[0])
+        nc.scalar.activation(w_out[:, CAST_SPLIT:, 2:4, :], w_in[1][:, CAST_SPLIT:], COPY)
+        nc.vector.tensor_copy(w_out[:, :CAST_SPLIT, 2:4, :], w_in[1][:, :CAST_SPLIT])
 
         x_sc = keep.tile([P, S], U8, name="x_sc", align_bytes=64)
         nc.vector.tensor_copy(x_sc[:], scales[:].indirect(offs_sb[:]))
@@ -77,66 +79,78 @@ def tile_picked_gae8_none_po_kernel(
                 x_codes[:, h * HALF : (h + 1) * HALF], words[:].bitcast(U32).indirect(offs_sb[:, cols])
             )
 
-        err = [win_y[(t - 1) % PACK][:, S:] for t in range(PACK)]
-        for u, h in ((0, 0), (0, 1), (1, 0), (1, 1)):
-            cols = slice(h * HALF, (h + 1) * HALF)
-            for t in (2 * u, 2 * u + 1):
-                y = psum.tile([P, HALF], F32, name=f"y{t}{h}")
-                nc.tensor.matmul_mx(
-                    out=y[:],
-                    lhsT=w_codes[:, t * P : (t + 1) * P].bitcast(FP8X4),
-                    lhsT_scale=w_sc[:, t * P : (t + 1) * P],
-                    rhs=x_codes[:, cols].bitcast(FP8X4),
-                    rhs_scale=x_sc[:, cols],
-                    start=True,
-                    stop=True,
-                )
-                nc.vector.tensor_tensor(err[t][:, cols], rw_sb[u][:, t % 2, cols], y[:], SUBTRACT)
-                nc.scalar.activation(win_y[t][:, cols], y[:], COPY, scale=GAMMA)
+        err = [win_y[PACK - 1 - t][:, S:] for t in range(PACK)]
+        pieces = [(t, h * HALF, HALF) for h in range(2) for t in range(2)] + [(t, 0, S) for t in range(2, PACK)]
+        for t, c0, width in pieces:
+            cols = slice(c0, c0 + width)
+            y = psum.tile([P, width], F32, name=f"y{t}_{c0}")
+            nc.tensor.matmul_mx(
+                out=y[:],
+                lhsT=w_codes[:, t * P : (t + 1) * P].bitcast(FP8X4),
+                lhsT_scale=w_sc[:, t * P : (t + 1) * P],
+                rhs=x_codes[:, cols].bitcast(FP8X4),
+                rhs_scale=x_sc[:, cols],
+                start=True,
+                stop=True,
+            )
+            nc.vector.tensor_tensor(err[t][:, cols], rw_sb[t][:, cols], y[:], SUBTRACT)
+            nc.scalar.activation(win_y[t][:, cols], y[:], COPY, scale=GAMMA)
 
         win_d = [keep.tile([P, 2 * S], F32, name=f"win_d{t}") for t in range(PACK)]
-        d_damped = [keep.tile([P, S], F32, name=f"d_damped{t}", tag=f"slot{t}", align_bytes=64) for t in range(PACK)]
         for t in range(PACK):
             nc.vector.tensor_tensor(win_d[t][:, S:], win_y[t][:].indirect(nx_sb[:]), err[t], ADD)
-            nc.scalar.activation(win_d[t][:, :S], win_d[t][:, S:], COPY, scale=DAMP * DAMP)
-            nc.scalar.activation(d_damped[t][:], win_d[t][:, S:], COPY, scale=DAMP)
+        d = [win_d[t][:, S:] for t in range(PACK)]
 
-        win_d2 = [keep.tile([P, S], F32, name=f"win_d2{t}") for t in range(PACK)]
-        for t in range(PACK):
-            nc.vector.tensor_tensor(win_d2[t][:], win_d[t][:].indirect(nx_sb[:]), d_damped[t][:], ADD)
+        win_d2 = [keep.tile([P, 2 * S if t < 2 else S], F32, name=f"win_d2{t}") for t in range(PACK)]
+        damped = [win_d2[t][:, S:] if t < 2 else keep.tile([P, S], F32, name=f"damped{t}")[:] for t in range(PACK)]
+        for ta in (0, 2):
+            tb = ta + 1
+            nc.scalar.activation(win_d[ta][:, :S], d[ta], COPY, scale=DAMP * DAMP)
+            nc.scalar.activation(win_d[tb][:, :S], d[tb], COPY, scale=DAMP * DAMP)
+            nc.scalar.activation(damped[tb][:, CHUNK:], d[tb][:, CHUNK:], COPY, scale=DAMP)
+            nc.scalar.activation(damped[ta], d[ta], COPY, scale=DAMP)
+            nc.scalar.activation(damped[tb][:, :CHUNK], d[tb][:, :CHUNK], COPY, scale=DAMP)
 
         out_rows = out_0.rearrange("(p t) c -> p t c", t=PACK)
         out_words = out_1[0].rearrange("p n t -> p (n t)").bitcast(I32)
+        res = [keep.tile([P, 2, S], F32, name=f"res{u}") for u in range(2)]
+        res_bf = keep.tile([P, S * PACK], BF16, name="res_bf", align_bytes=64)
+        dst = res_bf[:].rearrange("p (c i t) -> p c t i", i=4, t=PACK)
+        src = [res[u][:].rearrange("p t (c i) -> p c t i", i=4) for u in range(2)]
+
+        for t in (0, 1):
+            nc.vector.tensor_tensor(win_d2[t][:, :S], win_d[t][:].indirect(nx_sb[:]), damped[t], ADD)
+        for t in (0, 1):
+            nc.vector.tensor_tensor(res[0][:, t, :], win_d2[t][:].indirect(nx_sb[:]), d[t], ADD)
+        nc.sync.dma_start(out_rows[:, 0:2, :], res[0][:])
+        nc.scalar.copy(dst[:, :, 0:2, :], src[0])
+
+        for t in (2, 3):
+            nc.vector.tensor_tensor(win_d2[t][:], win_d[t][:].indirect(nx_sb[:]), damped[t], ADD)
+        o_codes = keep.tile([P, S], I32, name="o_codes", align_bytes=64)
         o_sc = keep.tile([P, S], U8, name="o_sc", align_bytes=64)
-        first = keep.tile([P, PACK, 2 * CHUNK], F32, name="res01", tag="slot3", align_bytes=64)
-        for c in range(S // CHUNK):
+        chunks = S // CHUNK
+        for c in range(chunks):
             c0, c1 = c * CHUNK, (c + 1) * CHUNK
-            if c < 2:
-                res = first[:, :, c0:c1]
-            else:
-                later = keep.tile([P, PACK, CHUNK], F32, name=f"res{c}", tag=f"bf{c - 2}", align_bytes=64)
-                res = later[:]
-            for t in range(PACK):
+            for t in (2, 3):
                 nc.vector.tensor_tensor(
-                    res[:, t, :],
+                    res[1][:, t - 2, c0:c1],
                     win_d2[t][:].indirect(nx_sb[:, c0 // LIST_ROWS : c1 // LIST_ROWS]),
-                    win_d[t][:, S + c0 : S + c1],
+                    d[t][:, c0:c1],
                     ADD,
                 )
-            if c == 1:
-                nc.sync.dma_start(out_rows[:, :, :c1], first[:])
-            elif c > 1:
-                nc.sync.dma_start(out_rows[:, :, c0:c1], res)
-            res_bf = keep.tile([P, CHUNK * PACK], BF16, name=f"res_bf{c}", tag=f"bf{c}", align_bytes=64)
-            dst = res_bf[:].rearrange("p (c i t) -> p c t i", i=4, t=PACK)
-            src = res.rearrange("p t (c i) -> p c t i", i=4)
-            if c < S // CHUNK - 1:
-                nc.scalar.copy(dst, src)
+            if c % 2 == 1:
+                nc.sync.dma_start(out_rows[:, 2:4, c0 - CHUNK : c1], res[1][:, :, c0 - CHUNK : c1])
+            groups = slice(c0 // 4, c1 // 4)
+            if c < chunks - 1:
+                nc.scalar.copy(dst[:, groups, 2:4, :], src[1][:, groups])
             else:
-                nc.vector.tensor_copy(dst, src)
-            o_codes = keep.tile([P, CHUNK], I32, name=f"o_codes{c}", align_bytes=64)
-            nc.vector.quantize_mx(out=o_codes[:].bitcast(FP8X4), scales=o_sc[:, c0:c1], in_=res_bf[:])
-            nc.sync.dma_start(out_words[:, c0:c1], o_codes[:])
+                nc.vector.tensor_copy(dst[:, groups, 2:4, :], src[1][:, groups])
+            nc.vector.quantize_mx(
+                out=o_codes[:, c0:c1].bitcast(FP8X4), scales=o_sc[:, c0:c1], in_=res_bf[:, PACK * c0 : PACK * c1]
+            )
+            if c % 2 == 1:
+                nc.sync.dma_start(out_words[:, c0 - CHUNK : c1], o_codes[:, c0 - CHUNK : c1])
         for q in range(4):
             queue = nc.scalar if q % 2 == 0 else nc.sync
             queue.dma_start(

@@ -18,12 +18,15 @@ SUBTRACT = mybir.AluOpType.subtract
 
 P = 128
 PACK = 4
+QUADRANTS = 4
 LIST_ROWS = 16
+LINE = 4
 HALF = S // 2
 GAMMA = 0.9
 DAMP = 0.75
-CHUNK = 128
 CAST_SPLIT = 32
+LAST_PIECE = 128
+EDGES = (0, 256, 384, 512)
 
 
 def tile_picked_gae8_none_po_kernel(
@@ -42,17 +45,19 @@ def tile_picked_gae8_none_po_kernel(
         scales = keep.tile([P, T], U8, name="scales")
         win_y = [keep.tile([P, 2 * S], F32, name=f"win_y{t}") for t in range(PACK)]
 
-        nc.vector.memset(scales[:].bitcast(I32), 0)
-        nc.sync.dma_start(offs_sb[:], offs)
+        nc.vector.memset(scales[:, : T // 2].bitcast(I32), 0)
+        nc.gpsimd.memset(scales[:, T // 2 :].bitcast(I32), 0)
+
         w_rows = w1.rearrange("(p j) c -> p j c", j=PACK)
         nc.sync.dma_start(w_raw[0][:], w_rows[:, 0:2, :])
-        nc.sync.dma_start(nx_sb[:], nx)
+        nc.sync.dma_start(offs_sb[:], offs)
         nc.sync.dma_start(w_raw[1][:], w_rows[:, 2:4, :])
-        for q in range(4):
+        for q in range(QUADRANTS):
             nc.sync.dma_start(
                 scales[32 * q : 32 * q + 4, :].bitcast(I32), x_scales[0, 4 * q : 4 * q + 4, :].bitcast(I32)
             )
         nc.sync.dma_start(words[:], x_words[0].rearrange("p n t -> p (n t)").bitcast(I32))
+        nc.sync.dma_start(nx_sb[:], nx)
         rw_rows = rw.rearrange("(p t) c -> p t c", t=PACK)
         rw_sb = [keep.tile([P, S], F32, name=f"rw_sb{t}") for t in range(PACK)]
         for t in range(PACK):
@@ -74,12 +79,12 @@ def tile_picked_gae8_none_po_kernel(
 
         x_codes = keep.tile([P, S], U32, name="x_codes", tag="operand", align_bytes=64)
         for h in range(2):
-            cols = slice(h * HALF // LIST_ROWS, (h + 1) * HALF // LIST_ROWS)
+            entries = slice(h * HALF // LIST_ROWS, (h + 1) * HALF // LIST_ROWS)
             nc.vector.tensor_copy(
-                x_codes[:, h * HALF : (h + 1) * HALF], words[:].bitcast(U32).indirect(offs_sb[:, cols])
+                x_codes[:, h * HALF : (h + 1) * HALF], words[:].bitcast(U32).indirect(offs_sb[:, entries])
             )
 
-        err = [win_y[PACK - 1 - t][:, S:] for t in range(PACK)]
+        diff = [win_y[PACK - 1 - t][:, S:] for t in range(PACK)]
         pieces = [(t, h * HALF, HALF) for h in range(2) for t in range(2)] + [(t, 0, S) for t in range(2, PACK)]
         for t, c0, width in pieces:
             cols = slice(c0, c0 + width)
@@ -93,12 +98,12 @@ def tile_picked_gae8_none_po_kernel(
                 start=True,
                 stop=True,
             )
-            nc.vector.tensor_tensor(err[t][:, cols], rw_sb[t][:, cols], y[:], SUBTRACT)
+            nc.vector.tensor_tensor(diff[t][:, cols], rw_sb[t][:, cols], y[:], SUBTRACT)
             nc.scalar.activation(win_y[t][:, cols], y[:], COPY, scale=GAMMA)
 
         win_d = [keep.tile([P, 2 * S], F32, name=f"win_d{t}") for t in range(PACK)]
         for t in range(PACK):
-            nc.vector.tensor_tensor(win_d[t][:, S:], win_y[t][:].indirect(nx_sb[:]), err[t], ADD)
+            nc.vector.tensor_tensor(win_d[t][:, S:], win_y[t][:].indirect(nx_sb[:]), diff[t], ADD)
         d = [win_d[t][:, S:] for t in range(PACK)]
 
         win_d2 = [keep.tile([P, 2 * S if t < 2 else S], F32, name=f"win_d2{t}") for t in range(PACK)]
@@ -107,31 +112,29 @@ def tile_picked_gae8_none_po_kernel(
             tb = ta + 1
             nc.scalar.activation(win_d[ta][:, :S], d[ta], COPY, scale=DAMP * DAMP)
             nc.scalar.activation(win_d[tb][:, :S], d[tb], COPY, scale=DAMP * DAMP)
-            nc.scalar.activation(damped[tb][:, CHUNK:], d[tb][:, CHUNK:], COPY, scale=DAMP)
+            nc.scalar.activation(damped[tb][:, LAST_PIECE:], d[tb][:, LAST_PIECE:], COPY, scale=DAMP)
             nc.scalar.activation(damped[ta], d[ta], COPY, scale=DAMP)
-            nc.scalar.activation(damped[tb][:, :CHUNK], d[tb][:, :CHUNK], COPY, scale=DAMP)
+            nc.scalar.activation(damped[tb][:, :LAST_PIECE], d[tb][:, :LAST_PIECE], COPY, scale=DAMP)
 
         out_rows = out_0.rearrange("(p t) c -> p t c", t=PACK)
         out_words = out_1[0].rearrange("p n t -> p (n t)").bitcast(I32)
         res = [keep.tile([P, 2, S], F32, name=f"res{u}") for u in range(2)]
         res_bf = keep.tile([P, S * PACK], BF16, name="res_bf", align_bytes=64)
-        dst = res_bf[:].rearrange("p (c i t) -> p c t i", i=4, t=PACK)
-        src = [res[u][:].rearrange("p t (c i) -> p c t i", i=4) for u in range(2)]
+        rounded = res_bf[:].rearrange("p (c i t) -> p c t i", i=LINE, t=PACK)
+        exact = [res[u][:].rearrange("p t (c i) -> p c t i", i=LINE) for u in range(2)]
 
         for t in (0, 1):
             nc.vector.tensor_tensor(win_d2[t][:, :S], win_d[t][:].indirect(nx_sb[:]), damped[t], ADD)
         for t in (0, 1):
             nc.vector.tensor_tensor(res[0][:, t, :], win_d2[t][:].indirect(nx_sb[:]), d[t], ADD)
         nc.sync.dma_start(out_rows[:, 0:2, :], res[0][:])
-        nc.scalar.copy(dst[:, :, 0:2, :], src[0])
+        nc.scalar.copy(rounded[:, :, 0:2, :], exact[0])
 
         for t in (2, 3):
             nc.vector.tensor_tensor(win_d2[t][:], win_d[t][:].indirect(nx_sb[:]), damped[t], ADD)
         o_codes = keep.tile([P, S], I32, name="o_codes", align_bytes=64)
         o_sc = keep.tile([P, S], U8, name="o_sc", align_bytes=64)
-        chunks = S // CHUNK
-        for c in range(chunks):
-            c0, c1 = c * CHUNK, (c + 1) * CHUNK
+        for c0, c1 in zip(EDGES[:-1], EDGES[1:]):
             for t in (2, 3):
                 nc.vector.tensor_tensor(
                     res[1][:, t - 2, c0:c1],
@@ -139,19 +142,21 @@ def tile_picked_gae8_none_po_kernel(
                     d[t][:, c0:c1],
                     ADD,
                 )
-            if c % 2 == 1:
-                nc.sync.dma_start(out_rows[:, 2:4, c0 - CHUNK : c1], res[1][:, :, c0 - CHUNK : c1])
-            groups = slice(c0 // 4, c1 // 4)
-            if c < chunks - 1:
-                nc.scalar.copy(dst[:, groups, 2:4, :], src[1][:, groups])
+            half_done = c1 % HALF == 0
+            if half_done:
+                nc.sync.dma_start(out_rows[:, 2:4, c1 - HALF : c1], res[1][:, :, c1 - HALF : c1])
+            groups = slice(c0 // LINE, c1 // LINE)
+            if c1 < S:
+                nc.scalar.copy(rounded[:, groups, 2:4, :], exact[1][:, groups])
             else:
-                nc.vector.tensor_copy(dst[:, groups, 2:4, :], src[1][:, groups])
+                nc.vector.tensor_copy(rounded[:, groups, 2:4, :], exact[1][:, groups])
             nc.vector.quantize_mx(
                 out=o_codes[:, c0:c1].bitcast(FP8X4), scales=o_sc[:, c0:c1], in_=res_bf[:, PACK * c0 : PACK * c1]
             )
-            if c % 2 == 1:
-                nc.sync.dma_start(out_words[:, c0 - CHUNK : c1], o_codes[:, c0 - CHUNK : c1])
-        for q in range(4):
+            if half_done:
+                nc.sync.dma_start(out_words[:, c1 - HALF : c1], o_codes[:, c1 - HALF : c1])
+
+        for q in range(QUADRANTS):
             queue = nc.scalar if q % 2 == 0 else nc.sync
             queue.dma_start(
                 out_2[0, 4 * q : 4 * q + 4, :].bitcast(I32), o_sc[32 * q : 32 * q + 4, :].bitcast(I32)

@@ -24,7 +24,6 @@ LINE = 4
 HALF = S // 2
 GAMMA = 0.9
 DAMP = 0.75
-CAST_SPLIT = 32
 LAST_PIECE = 128
 EDGES = (0, 256, 384, 512)
 
@@ -51,11 +50,11 @@ def tile_picked_gae8_none_po_kernel(
         w_rows = w1.rearrange("(p j) c -> p j c", j=PACK)
         nc.sync.dma_start(w_raw[0][:], w_rows[:, 0:2, :])
         nc.sync.dma_start(offs_sb[:], offs)
-        nc.sync.dma_start(w_raw[1][:], w_rows[:, 2:4, :])
         for q in range(QUADRANTS):
             nc.sync.dma_start(
                 scales[32 * q : 32 * q + 4, :].bitcast(I32), x_scales[0, 4 * q : 4 * q + 4, :].bitcast(I32)
             )
+        nc.sync.dma_start(w_raw[1][:], w_rows[:, 2:4, :])
         nc.sync.dma_start(words[:], x_words[0].rearrange("p n t -> p (n t)").bitcast(I32))
         nc.sync.dma_start(nx_sb[:], nx)
         rw_rows = rw.rearrange("(p t) c -> p t c", t=PACK)
@@ -66,12 +65,15 @@ def tile_picked_gae8_none_po_kernel(
         w_bf = keep.tile([P, N * PACK], BF16, name="w_bf", tag="operand", align_bytes=64)
         w_out = w_bf[:].rearrange("p (t m j) -> p m j t", t=PACK, j=PACK)
         w_in = [w_raw[h][:].rearrange("p j (m t) -> p m j t", t=PACK) for h in range(2)]
-        nc.vector.tensor_copy(w_out[:, :, 0:2, :], w_in[0])
-        nc.scalar.activation(w_out[:, CAST_SPLIT:, 2:4, :], w_in[1][:, CAST_SPLIT:], COPY)
-        nc.vector.tensor_copy(w_out[:, :CAST_SPLIT, 2:4, :], w_in[1][:, :CAST_SPLIT])
 
+        def round_weights(h):
+            nc.vector.tensor_copy(w_out[:, : P // 2, 2 * h : 2 * h + 2, :], w_in[h][:, : P // 2])
+            nc.scalar.activation(w_out[:, P // 2 :, 2 * h : 2 * h + 2, :], w_in[h][:, P // 2 :], COPY)
+
+        round_weights(0)
         x_sc = keep.tile([P, S], U8, name="x_sc", align_bytes=64)
         nc.vector.tensor_copy(x_sc[:], scales[:].indirect(offs_sb[:]))
+        round_weights(1)
 
         w_codes = keep.tile([P, N], U32, name="w_codes", align_bytes=64)
         w_sc = keep.tile([P, N], U8, name="w_sc", align_bytes=64)

@@ -50,10 +50,8 @@ def tile_picked_gae8_none_po_kernel(
         w_rows = w1.rearrange("(p j) c -> p j c", j=PACK)
         nc.sync.dma_start(w_raw[0][:], w_rows[:, 0:2, :])
         nc.sync.dma_start(offs_sb[:], offs)
-        for q in range(QUADRANTS):
-            nc.sync.dma_start(
-                scales[32 * q : 32 * q + 4, :].bitcast(I32), x_scales[0, 4 * q : 4 * q + 4, :].bitcast(I32)
-            )
+        for r in range(4):
+            nc.sync.dma_start(scales[r:P:32, :].bitcast(I32), x_scales[0, r:16:4, :].bitcast(I32))
         nc.sync.dma_start(w_raw[1][:], w_rows[:, 2:4, :])
         nc.sync.dma_start(words[:], x_words[0].rearrange("p n t -> p (n t)").bitcast(I32))
         nc.sync.dma_start(nx_sb[:], nx)
@@ -158,8 +156,6 @@ def tile_picked_gae8_none_po_kernel(
             if half_done:
                 nc.sync.dma_start(out_words[:, c1 - HALF : c1], o_codes[:, c1 - HALF : c1])
 
-        for q in range(QUADRANTS):
-            queue = nc.scalar if q % 2 == 0 else nc.sync
-            queue.dma_start(
-                out_2[0, 4 * q : 4 * q + 4, :].bitcast(I32), o_sc[32 * q : 32 * q + 4, :].bitcast(I32)
-            )
+        for r in range(4):
+            queue = nc.scalar if r % 2 == 0 else nc.sync
+            queue.dma_start(out_2[0, r:16:4, :].bitcast(I32), o_sc[r:P:32, :].bitcast(I32))

@@ -1,6 +1,7 @@
 from contextlib import ExitStack
 
 import concourse.mybir as mybir
+from concourse.masks import make_identity
 
 K, T, S, N = 512, 2048, 512, 512
 FLOPS = 2 * K * N * S
@@ -24,7 +25,7 @@ LINE = 4
 HALF = S // 2
 GAMMA = 0.9
 DAMP = 0.75
-LAST_PIECE = 128
+LAST_PIECE = 32
 EDGES = (0, 256, 384, 512)
 
 
@@ -56,9 +57,9 @@ def tile_picked_gae8_none_po_kernel(
         nc.sync.dma_start(words[:], x_words[0].rearrange("p n t -> p (n t)").bitcast(I32))
         nc.sync.dma_start(nx_sb[:], nx)
         rw_rows = rw.rearrange("(p t) c -> p t c", t=PACK)
-        rw_sb = [keep.tile([P, S], F32, name=f"rw_sb{t}") for t in range(PACK)]
+        rw_sb = [win_y[t][:, S:] if t < 3 else keep.tile([P, S], F32, name=f"rw_sb{t}")[:] for t in range(PACK)]
         for t in range(PACK):
-            nc.sync.dma_start(rw_sb[t][:], rw_rows[:, t, :])
+            nc.sync.dma_start(rw_sb[t], rw_rows[:, t, :])
 
         w_bf = keep.tile([P, N * PACK], BF16, name="w_bf", tag="operand", align_bytes=64)
         w_out = w_bf[:].rearrange("p (t m j) -> p m j t", t=PACK, j=PACK)
@@ -84,13 +85,12 @@ def tile_picked_gae8_none_po_kernel(
                 x_codes[:, h * HALF : (h + 1) * HALF], words[:].bitcast(U32).indirect(offs_sb[:, entries])
             )
 
-        diff = [win_y[PACK - 1 - t][:, S:] for t in range(PACK)]
-        pieces = [(t, h * HALF, HALF) for h in range(2) for t in range(2)] + [(t, 0, S) for t in range(2, PACK)]
-        for t, c0, width in pieces:
-            cols = slice(c0, c0 + width)
-            y = psum.tile([P, width], F32, name=f"y{t}_{c0}")
+        ident = keep.tile([P, P], F32, name="ident")
+        make_identity(nc, ident[:])
+
+        def product(y, t, cols):
             nc.tensor.matmul_mx(
-                out=y[:],
+                out=y,
                 lhsT=w_codes[:, t * P : (t + 1) * P].bitcast(FP8X4),
                 lhsT_scale=w_sc[:, t * P : (t + 1) * P],
                 rhs=x_codes[:, cols].bitcast(FP8X4),
@@ -98,23 +98,36 @@ def tile_picked_gae8_none_po_kernel(
                 start=True,
                 stop=True,
             )
-            nc.vector.tensor_tensor(diff[t][:, cols], rw_sb[t][:, cols], y[:], SUBTRACT)
-            nc.scalar.activation(win_y[t][:, cols], y[:], COPY, scale=GAMMA)
 
         win_d = [keep.tile([P, 2 * S], F32, name=f"win_d{t}") for t in range(PACK)]
-        for t in range(PACK):
-            nc.vector.tensor_tensor(win_d[t][:, S:], win_y[t][:].indirect(nx_sb[:]), diff[t], ADD)
-        d = [win_d[t][:, S:] for t in range(PACK)]
-
-        win_d2 = [keep.tile([P, 2 * S if t < 2 else S], F32, name=f"win_d2{t}") for t in range(PACK)]
-        damped = [win_d2[t][:, S:] if t < 2 else keep.tile([P, S], F32, name=f"damped{t}")[:] for t in range(PACK)]
-        for ta in (0, 2):
-            tb = ta + 1
-            nc.scalar.activation(win_d[ta][:, :S], d[ta], COPY, scale=DAMP * DAMP)
-            nc.scalar.activation(win_d[tb][:, :S], d[tb], COPY, scale=DAMP * DAMP)
-            nc.scalar.activation(damped[tb][:, LAST_PIECE:], d[tb][:, LAST_PIECE:], COPY, scale=DAMP)
-            nc.scalar.activation(damped[ta], d[ta], COPY, scale=DAMP)
-            nc.scalar.activation(damped[tb][:, :LAST_PIECE], d[tb][:, :LAST_PIECE], COPY, scale=DAMP)
+        diff = [win_d[t][:, S:] for t in range(PACK)]
+        for h in range(2):
+            for t in range(2):
+                cols = slice(h * HALF, (h + 1) * HALF)
+                y = psum.tile([P, HALF], F32, name=f"y{t}_{h}", tag=f"bank{t}_{h}")
+                product(y[:], t, cols)
+                nc.vector.tensor_tensor(diff[t][:, cols], rw_sb[t][:, cols], y[:], SUBTRACT)
+                nc.scalar.activation(win_y[t][:, cols], y[:], COPY, scale=GAMMA)
+        y = psum.tile([P, S], F32, name="y2", tag="bank2")
+        product(y[:], 2, slice(0, S))
+        nc.vector.tensor_tensor(diff[2], rw_sb[2], y[:], SUBTRACT)
+        nc.scalar.activation(win_y[2][:, :S], y[:], COPY, scale=GAMMA)
+        y = psum.tile([P, S], F32, name="y3", tag="bank0_1")
+        product(y[:], 3, slice(0, S))
+        minus_y = win_y[3][:, S:]
+        nc.scalar.activation(minus_y, y[:], COPY, scale=-1.0)
+        turned = psum.tile([P, S], F32, name="turned")
+        for n, term in enumerate((rw_sb[3], minus_y)):
+            for b in range(S // P):
+                cols = slice(b * P, (b + 1) * P)
+                nc.tensor.matmul(
+                    turned[:, cols],
+                    term[:, cols],
+                    ident[:],
+                    start=(n == 0 and b == 0),
+                    stop=(n == 1 and b == S // P - 1),
+                    is_transpose=True,
+                )
 
         out_rows = out_0.rearrange("(p t) c -> p t c", t=PACK)
         out_words = out_1[0].rearrange("p n t -> p (n t)").bitcast(I32)
@@ -123,16 +136,50 @@ def tile_picked_gae8_none_po_kernel(
         rounded = res_bf[:].rearrange("p (c i t) -> p c t i", i=LINE, t=PACK)
         exact = [res[u][:].rearrange("p t (c i) -> p c t i", i=LINE) for u in range(2)]
 
-        for t in (0, 1):
-            nc.vector.tensor_tensor(win_d2[t][:, :S], win_d[t][:].indirect(nx_sb[:]), damped[t], ADD)
-        for t in (0, 1):
-            nc.vector.tensor_tensor(res[0][:, t, :], win_d2[t][:].indirect(nx_sb[:]), d[t], ADD)
-        nc.sync.dma_start(out_rows[:, 0:2, :], res[0][:])
-        nc.scalar.copy(rounded[:, :, 0:2, :], exact[0])
+        d = [keep.tile([P, S], F32, name=f"d{t}")[:] for t in range(PACK)]
+        win_d2 = [
+            keep.tile([P, 2 * S if t < 2 else S], F32, name=f"win_d2{t}", tag=f"win_d2{t}", align_bytes=64)
+            for t in range(PACK)
+        ]
+        d2 = [win_d2[t][:, S:] if t < 2 else keep.tile([P, S], F32, name=f"d2{t}")[:] for t in range(3)]
+        damped = keep.tile([P, S], F32, name="damped")
+        turned_sb = win_d[2][:, :S]
+        back = psum.tile([P, S], F32, name="back")
 
-        for t in (2, 3):
-            nc.vector.tensor_tensor(win_d2[t][:], win_d[t][:].indirect(nx_sb[:]), damped[t], ADD)
-        o_codes = keep.tile([P, S], I32, name="o_codes", align_bytes=64)
+        def second_step(t):
+            nc.scalar.activation(win_d[t][:, :S], d[t], COPY, scale=DAMP)
+            nc.vector.tensor_tensor(d2[t], win_d[t][:].indirect(nx_sb[:]), d[t], ADD)
+
+        def last_step(t):
+            nc.scalar.activation(win_d2[t][:, :S], d2[t], COPY, scale=DAMP)
+            nc.vector.tensor_tensor(res[0][:, t, :], win_d2[t][:].indirect(nx_sb[:]), d[t], ADD)
+
+        for t in range(3):
+            nc.vector.tensor_tensor(d[t], win_y[t][:].indirect(nx_sb[:]), diff[t], ADD)
+        second_step(0)
+        second_step(1)
+        nc.scalar.activation(turned_sb, turned[:], COPY)
+        for b in range(S // P):
+            cols = slice(b * P, (b + 1) * P)
+            nc.tensor.transpose(back[:, cols], turned_sb[:, cols], ident[:])
+        nc.scalar.activation(win_y[3][:, :S], minus_y, COPY, scale=-GAMMA * DAMP * DAMP)
+        last_step(0)
+        last_step(1)
+        nc.sync.dma_start(out_rows[:, 0:2, :], res[0][:])
+        nc.scalar.activation(diff[3], back[:], COPY, scale=DAMP * DAMP)
+        nc.vector.tensor_tensor(win_d[3][:, :S], win_y[3][:].indirect(nx_sb[:]), diff[3], ADD)
+        second_step(2)
+        early = EDGES[-2] // LINE
+        nc.scalar.copy(rounded[:, :early, 0:2, :], exact[0][:, :early])
+        nc.scalar.activation(damped[:], win_d[3][:, :S], COPY, scale=1.0 / DAMP)
+        nc.vector.tensor_tensor(win_d2[3][:], win_d[3][:].indirect(nx_sb[:]), damped[:], ADD)
+        d_out = d[3].rearrange("p (g c) -> p g c", c=P)
+        d_in = win_d[3][:, :S].rearrange("p (g c) -> p g c", c=P)
+        nc.scalar.activation(d_out[:, :, LAST_PIECE:], d_in[:, :, LAST_PIECE:], COPY, scale=1.0 / (DAMP * DAMP))
+        nc.scalar.activation(win_d2[2][:], d2[2], COPY, scale=DAMP)
+        nc.scalar.activation(d_out[:, :, :LAST_PIECE], d_in[:, :, :LAST_PIECE], COPY, scale=1.0 / (DAMP * DAMP))
+        nc.scalar.copy(rounded[:, early:, 0:2, :], exact[0][:, early:])
+        o_codes = keep.tile([P, S], I32, name="o_codes", tag="win_d22", align_bytes=64)
         o_sc = keep.tile([P, S], U8, name="o_sc", align_bytes=64)
         for c0, c1 in zip(EDGES[:-1], EDGES[1:]):
             for t in (2, 3):
@@ -150,10 +197,11 @@ def tile_picked_gae8_none_po_kernel(
                 nc.scalar.copy(rounded[:, groups, 2:4, :], exact[1][:, groups])
             else:
                 nc.vector.tensor_copy(rounded[:, groups, 2:4, :], exact[1][:, groups])
+        for c0, c1 in zip(EDGES[:-1], EDGES[1:]):
             nc.vector.quantize_mx(
                 out=o_codes[:, c0:c1].bitcast(FP8X4), scales=o_sc[:, c0:c1], in_=res_bf[:, PACK * c0 : PACK * c1]
             )
-            if half_done:
+            if c1 % HALF == 0:
                 nc.sync.dma_start(out_words[:, c1 - HALF : c1], o_codes[:, c1 - HALF : c1])
 
         for r in range(4):

@@ -57,7 +57,7 @@ def tile_picked_gae8_none_po_kernel(
         nc.sync.dma_start(words[:], x_words[0].rearrange("p n t -> p (n t)").bitcast(I32))
         nc.sync.dma_start(nx_sb[:], nx)
         rw_rows = rw.rearrange("(p t) c -> p t c", t=PACK)
-        rw_sb = [win_y[t][:, S:] if t < 3 else keep.tile([P, S], F32, name=f"rw_sb{t}")[:] for t in range(PACK)]
+        rw_sb = [win_y[t][:, S:] if t < 2 else keep.tile([P, S], F32, name=f"rw_sb{t}")[:] for t in range(PACK)]
         for t in range(PACK):
             nc.sync.dma_start(rw_sb[t], rw_rows[:, t, :])
 
@@ -108,26 +108,25 @@ def tile_picked_gae8_none_po_kernel(
                 product(y[:], t, cols)
                 nc.vector.tensor_tensor(diff[t][:, cols], rw_sb[t][:, cols], y[:], SUBTRACT)
                 nc.scalar.activation(win_y[t][:, cols], y[:], COPY, scale=GAMMA)
-        y = psum.tile([P, S], F32, name="y2", tag="bank2")
-        product(y[:], 2, slice(0, S))
-        nc.vector.tensor_tensor(diff[2], rw_sb[2], y[:], SUBTRACT)
-        nc.scalar.activation(win_y[2][:, :S], y[:], COPY, scale=GAMMA)
-        y = psum.tile([P, S], F32, name="y3", tag="bank0_1")
-        product(y[:], 3, slice(0, S))
-        minus_y = win_y[3][:, S:]
-        nc.scalar.activation(minus_y, y[:], COPY, scale=-1.0)
-        turned = psum.tile([P, S], F32, name="turned")
-        for n, term in enumerate((rw_sb[3], minus_y)):
-            for b in range(S // P):
-                cols = slice(b * P, (b + 1) * P)
-                nc.tensor.matmul(
-                    turned[:, cols],
-                    term[:, cols],
-                    ident[:],
-                    start=(n == 0 and b == 0),
-                    stop=(n == 1 and b == S // P - 1),
-                    is_transpose=True,
-                )
+        minus_y = {t: win_y[t][:, S:] for t in (2, 3)}
+        turned = {}
+
+        def turn(t):
+            y = psum.tile([P, S], F32, name=f"y{t}", tag=f"bank{t - 2}_1")
+            product(y[:], t, slice(0, S))
+            nc.scalar.activation(minus_y[t], y[:], COPY, scale=-1.0)
+            turned[t] = psum.tile([P, S], F32, name=f"turned{t}")
+            for n, term in enumerate((rw_sb[t], minus_y[t])):
+                for b in range(S // P):
+                    cols = slice(b * P, (b + 1) * P)
+                    nc.tensor.matmul(
+                        turned[t][:, cols],
+                        term[:, cols],
+                        ident[:],
+                        start=(n == 0 and b == 0),
+                        stop=(n == 1 and b == S // P - 1),
+                        is_transpose=True,
+                    )
 
         out_rows = out_0.rearrange("(p t) c -> p t c", t=PACK)
         out_words = out_1[0].rearrange("p n t -> p (n t)").bitcast(I32)
@@ -141,10 +140,17 @@ def tile_picked_gae8_none_po_kernel(
             keep.tile([P, 2 * S if t < 2 else S], F32, name=f"win_d2{t}", tag=f"win_d2{t}", align_bytes=64)
             for t in range(PACK)
         ]
-        d2 = [win_d2[t][:, S:] if t < 2 else keep.tile([P, S], F32, name=f"d2{t}")[:] for t in range(3)]
-        damped = keep.tile([P, S], F32, name="damped")
-        turned_sb = win_d[2][:, :S]
-        back = psum.tile([P, S], F32, name="back")
+        d2 = [win_d2[t][:, S:] for t in range(2)]
+        damped = {t: keep.tile([P, S], F32, name=f"damped{t}") for t in (2, 3)}
+        back = {}
+
+        def turn_back(t):
+            turned_sb = keep.tile([P, S], F32, name=f"turned_sb{t}")
+            nc.scalar.activation(turned_sb[:], turned[t][:], COPY)
+            back[t] = psum.tile([P, S], F32, name=f"back{t}")
+            for b in range(S // P):
+                cols = slice(b * P, (b + 1) * P)
+                nc.tensor.transpose(back[t][:, cols], turned_sb[:, cols], ident[:])
 
         def second_step(t):
             nc.scalar.activation(win_d[t][:, :S], d[t], COPY, scale=DAMP)
@@ -154,31 +160,30 @@ def tile_picked_gae8_none_po_kernel(
             nc.scalar.activation(win_d2[t][:, :S], d2[t], COPY, scale=DAMP)
             nc.vector.tensor_tensor(res[0][:, t, :], win_d2[t][:].indirect(nx_sb[:]), d[t], ADD)
 
-        for t in range(3):
+        for t in range(2):
             nc.vector.tensor_tensor(d[t], win_y[t][:].indirect(nx_sb[:]), diff[t], ADD)
-        second_step(0)
-        second_step(1)
-        nc.scalar.activation(turned_sb, turned[:], COPY)
-        for b in range(S // P):
-            cols = slice(b * P, (b + 1) * P)
-            nc.tensor.transpose(back[:, cols], turned_sb[:, cols], ident[:])
-        nc.scalar.activation(win_y[3][:, :S], minus_y, COPY, scale=-GAMMA * DAMP * DAMP)
-        last_step(0)
-        last_step(1)
+        for t in range(2):
+            turn(t + 2)
+            second_step(t)
+        for t in range(2):
+            turn_back(t + 2)
+            last_step(t)
         nc.sync.dma_start(out_rows[:, 0:2, :], res[0][:])
-        nc.scalar.activation(diff[3], back[:], COPY, scale=DAMP * DAMP)
-        nc.vector.tensor_tensor(win_d[3][:, :S], win_y[3][:].indirect(nx_sb[:]), diff[3], ADD)
-        second_step(2)
-        early = EDGES[-2] // LINE
-        nc.scalar.copy(rounded[:, :early, 0:2, :], exact[0][:, :early])
-        nc.scalar.activation(damped[:], win_d[3][:, :S], COPY, scale=1.0 / DAMP)
-        nc.vector.tensor_tensor(win_d2[3][:], win_d[3][:].indirect(nx_sb[:]), damped[:], ADD)
+        for t in (2, 3):
+            nc.scalar.activation(win_y[t][:, :S], minus_y[t], COPY, scale=-GAMMA * DAMP * DAMP)
+            nc.scalar.activation(diff[t], back[t][:], COPY, scale=DAMP * DAMP)
+            nc.vector.tensor_tensor(win_d[t][:, :S], win_y[t][:].indirect(nx_sb[:]), diff[t], ADD)
+        for t in (2, 3):
+            nc.scalar.activation(damped[t][:], win_d[t][:, :S], COPY, scale=1.0 / DAMP)
+            nc.vector.tensor_tensor(win_d2[t][:], win_d[t][:].indirect(nx_sb[:]), damped[t][:], ADD)
+            if t == 2:
+                nc.scalar.copy(rounded[:, : HALF // LINE, 0:2, :], exact[0][:, : HALF // LINE])
         d_out = d[3].rearrange("p (g c) -> p g c", c=P)
         d_in = win_d[3][:, :S].rearrange("p (g c) -> p g c", c=P)
         nc.scalar.activation(d_out[:, :, LAST_PIECE:], d_in[:, :, LAST_PIECE:], COPY, scale=1.0 / (DAMP * DAMP))
-        nc.scalar.activation(win_d2[2][:], d2[2], COPY, scale=DAMP)
+        nc.scalar.activation(d[2], win_d[2][:, :S], COPY, scale=1.0 / (DAMP * DAMP))
         nc.scalar.activation(d_out[:, :, :LAST_PIECE], d_in[:, :, :LAST_PIECE], COPY, scale=1.0 / (DAMP * DAMP))
-        nc.scalar.copy(rounded[:, early:, 0:2, :], exact[0][:, early:])
+        nc.scalar.copy(rounded[:, HALF // LINE :, 0:2, :], exact[0][:, HALF // LINE :])
         o_codes = keep.tile([P, S], I32, name="o_codes", tag="win_d22", align_bytes=64)
         o_sc = keep.tile([P, S], U8, name="o_sc", align_bytes=64)
         for c0, c1 in zip(EDGES[:-1], EDGES[1:]):

@@ -19,12 +19,15 @@ SUBTRACT = mybir.AluOpType.subtract
 
 P = 128
 PACK = 4
-QUADRANTS = 4
+QUADRANT = 32
+SCALE_ROWS = 4
+BLOCKS = 16
 LIST_ROWS = 16
 LINE = 4
 HALF = S // 2
 GAMMA = 0.9
 DAMP = 0.75
+EARLY, LATE = (0, 1), (2, 3)
 LAST_PIECE = 32
 EDGES = (0, 256, 384, 512)
 
@@ -51,13 +54,13 @@ def tile_picked_gae8_none_po_kernel(
         w_rows = w1.rearrange("(p j) c -> p j c", j=PACK)
         nc.sync.dma_start(w_raw[0][:], w_rows[:, 0:2, :])
         nc.sync.dma_start(offs_sb[:], offs)
-        for r in range(4):
-            nc.sync.dma_start(scales[r:P:32, :].bitcast(I32), x_scales[0, r:16:4, :].bitcast(I32))
+        for r in range(SCALE_ROWS):
+            nc.sync.dma_start(scales[r:P:QUADRANT, :].bitcast(I32), x_scales[0, r:BLOCKS:SCALE_ROWS, :].bitcast(I32))
         nc.sync.dma_start(w_raw[1][:], w_rows[:, 2:4, :])
         nc.sync.dma_start(words[:], x_words[0].rearrange("p n t -> p (n t)").bitcast(I32))
         nc.sync.dma_start(nx_sb[:], nx)
         rw_rows = rw.rearrange("(p t) c -> p t c", t=PACK)
-        rw_sb = [win_y[t][:, S:] if t < 2 else keep.tile([P, S], F32, name=f"rw_sb{t}")[:] for t in range(PACK)]
+        rw_sb = [win_y[t][:, S:] if t in EARLY else keep.tile([P, S], F32, name=f"rw_sb{t}")[:] for t in range(PACK)]
         for t in range(PACK):
             nc.sync.dma_start(rw_sb[t], rw_rows[:, t, :])
 
@@ -101,14 +104,16 @@ def tile_picked_gae8_none_po_kernel(
 
         win_d = [keep.tile([P, 2 * S], F32, name=f"win_d{t}") for t in range(PACK)]
         diff = [win_d[t][:, S:] for t in range(PACK)]
+
         for h in range(2):
-            for t in range(2):
+            for t in EARLY:
                 cols = slice(h * HALF, (h + 1) * HALF)
                 y = psum.tile([P, HALF], F32, name=f"y{t}_{h}", tag=f"bank{t}_{h}")
                 product(y[:], t, cols)
                 nc.vector.tensor_tensor(diff[t][:, cols], rw_sb[t][:, cols], y[:], SUBTRACT)
                 nc.scalar.activation(win_y[t][:, cols], y[:], COPY, scale=GAMMA)
-        minus_y = {t: win_y[t][:, S:] for t in (2, 3)}
+
+        minus_y = {t: win_y[t][:, S:] for t in LATE}
         turned = {}
 
         def turn(t):
@@ -137,11 +142,11 @@ def tile_picked_gae8_none_po_kernel(
 
         d = [keep.tile([P, S], F32, name=f"d{t}")[:] for t in range(PACK)]
         win_d2 = [
-            keep.tile([P, 2 * S if t < 2 else S], F32, name=f"win_d2{t}", tag=f"win_d2{t}", align_bytes=64)
+            keep.tile([P, 2 * S if t in EARLY else S], F32, name=f"win_d2{t}", tag=f"last{t}", align_bytes=64)
             for t in range(PACK)
         ]
-        d2 = [win_d2[t][:, S:] for t in range(2)]
-        damped = {t: keep.tile([P, S], F32, name=f"damped{t}") for t in (2, 3)}
+        d2 = [win_d2[t][:, S:] for t in EARLY]
+        damped = {t: keep.tile([P, S], F32, name=f"damped{t}") for t in LATE}
         back = {}
 
         def turn_back(t):
@@ -160,55 +165,59 @@ def tile_picked_gae8_none_po_kernel(
             nc.scalar.activation(win_d2[t][:, :S], d2[t], COPY, scale=DAMP)
             nc.vector.tensor_tensor(res[0][:, t, :], win_d2[t][:].indirect(nx_sb[:]), d[t], ADD)
 
-        for t in range(2):
+        for t in EARLY:
             nc.vector.tensor_tensor(d[t], win_y[t][:].indirect(nx_sb[:]), diff[t], ADD)
-        for t in range(2):
+        for t in EARLY:
             turn(t + 2)
             second_step(t)
-        for t in range(2):
+        for t in EARLY:
             turn_back(t + 2)
             last_step(t)
         nc.sync.dma_start(out_rows[:, 0:2, :], res[0][:])
-        for t in (2, 3):
+
+        for t in LATE:
             nc.scalar.activation(win_y[t][:, :S], minus_y[t], COPY, scale=-GAMMA * DAMP * DAMP)
             nc.scalar.activation(diff[t], back[t][:], COPY, scale=DAMP * DAMP)
             nc.vector.tensor_tensor(win_d[t][:, :S], win_y[t][:].indirect(nx_sb[:]), diff[t], ADD)
-        for t in (2, 3):
+
+        spans = list(zip(EDGES[:-1], EDGES[1:]))
+        groups = [slice(c0 // LINE, c1 // LINE) for c0, c1 in spans]
+        for t in LATE:
+            nc.scalar.copy(rounded[:, groups[t - 2], 0:2, :], exact[0][:, groups[t - 2]])
             nc.scalar.activation(damped[t][:], win_d[t][:, :S], COPY, scale=1.0 / DAMP)
             nc.vector.tensor_tensor(win_d2[t][:], win_d[t][:].indirect(nx_sb[:]), damped[t][:], ADD)
-            if t == 2:
-                nc.scalar.copy(rounded[:, : HALF // LINE, 0:2, :], exact[0][:, : HALF // LINE])
+
         d_out = d[3].rearrange("p (g c) -> p g c", c=P)
         d_in = win_d[3][:, :S].rearrange("p (g c) -> p g c", c=P)
         nc.scalar.activation(d_out[:, :, LAST_PIECE:], d_in[:, :, LAST_PIECE:], COPY, scale=1.0 / (DAMP * DAMP))
         nc.scalar.activation(d[2], win_d[2][:, :S], COPY, scale=1.0 / (DAMP * DAMP))
         nc.scalar.activation(d_out[:, :, :LAST_PIECE], d_in[:, :, :LAST_PIECE], COPY, scale=1.0 / (DAMP * DAMP))
-        nc.scalar.copy(rounded[:, HALF // LINE :, 0:2, :], exact[0][:, HALF // LINE :])
-        o_codes = keep.tile([P, S], I32, name="o_codes", tag="win_d22", align_bytes=64)
-        o_sc = keep.tile([P, S], U8, name="o_sc", align_bytes=64)
-        for c0, c1 in zip(EDGES[:-1], EDGES[1:]):
-            for t in (2, 3):
+        nc.scalar.copy(rounded[:, groups[2], 0:2, :], exact[0][:, groups[2]])
+
+        for (c0, c1), group in zip(spans, groups):
+            for t in LATE:
                 nc.vector.tensor_tensor(
                     res[1][:, t - 2, c0:c1],
                     win_d2[t][:].indirect(nx_sb[:, c0 // LIST_ROWS : c1 // LIST_ROWS]),
                     d[t][:, c0:c1],
                     ADD,
                 )
-            half_done = c1 % HALF == 0
-            if half_done:
+            if c1 % HALF == 0:
                 nc.sync.dma_start(out_rows[:, 2:4, c1 - HALF : c1], res[1][:, :, c1 - HALF : c1])
-            groups = slice(c0 // LINE, c1 // LINE)
             if c1 < S:
-                nc.scalar.copy(rounded[:, groups, 2:4, :], exact[1][:, groups])
+                nc.scalar.copy(rounded[:, group, 2:4, :], exact[1][:, group])
             else:
-                nc.vector.tensor_copy(rounded[:, groups, 2:4, :], exact[1][:, groups])
-        for c0, c1 in zip(EDGES[:-1], EDGES[1:]):
+                nc.vector.tensor_copy(rounded[:, group, 2:4, :], exact[1][:, group])
+
+        o_codes = keep.tile([P, S], I32, name="o_codes", tag="last2", align_bytes=64)
+        o_sc = keep.tile([P, S], U8, name="o_sc", align_bytes=64)
+        for c0, c1 in spans:
             nc.vector.quantize_mx(
                 out=o_codes[:, c0:c1].bitcast(FP8X4), scales=o_sc[:, c0:c1], in_=res_bf[:, PACK * c0 : PACK * c1]
             )
             if c1 % HALF == 0:
                 nc.sync.dma_start(out_words[:, c1 - HALF : c1], o_codes[:, c1 - HALF : c1])
 
-        for r in range(4):
+        for r in range(SCALE_ROWS):
             queue = nc.scalar if r % 2 == 0 else nc.sync
-            queue.dma_start(out_2[0, r:16:4, :].bitcast(I32), o_sc[r:P:32, :].bitcast(I32))
+            queue.dma_start(out_2[0, r:BLOCKS:SCALE_ROWS, :].bitcast(I32), o_sc[r:P:QUADRANT, :].bitcast(I32))

@@ -48,8 +48,7 @@ def tile_picked_gae8_none_po_kernel(
         scales = keep.tile([P, T], U8, name="scales")
         win_y = [keep.tile([P, 2 * S], F32, name=f"win_y{t}") for t in range(PACK)]
 
-        nc.vector.memset(scales[:, : T // 2].bitcast(I32), 0)
-        nc.gpsimd.memset(scales[:, T // 2 :].bitcast(I32), 0)
+        nc.vector.memset(scales[:].bitcast(I32), 0)
 
         w_rows = w1.rearrange("(p j) c -> p j c", j=PACK)
         nc.sync.dma_start(w_raw[0][:], w_rows[:, 0:2, :])
@@ -89,7 +88,8 @@ def tile_picked_gae8_none_po_kernel(
             )
 
         ident = keep.tile([P, P], F32, name="ident")
-        make_identity(nc, ident[:])
+        nc.vector.memset(ident[:], 0.0)
+        make_identity(nc, ident[:], nomemset=True)
 
         def product(y, t, cols):
             nc.tensor.matmul_mx(

@@ -204,10 +204,7 @@ def tile_picked_gae8_none_po_kernel(
                 )
             if c1 % HALF == 0:
                 nc.sync.dma_start(out_rows[:, 2:4, c1 - HALF : c1], res[1][:, :, c1 - HALF : c1])
-            if c1 < S:
-                nc.scalar.copy(rounded[:, group, 2:4, :], exact[1][:, group])
-            else:
-                nc.vector.tensor_copy(rounded[:, group, 2:4, :], exact[1][:, group])
+            nc.scalar.copy(rounded[:, group, 2:4, :], exact[1][:, group])
 
         o_codes = keep.tile([P, S], I32, name="o_codes", tag="last2", align_bytes=64)
         o_sc = keep.tile([P, S], U8, name="o_sc", align_bytes=64)

@@ -45,23 +45,26 @@ def tile_picked_gae8_none_po_kernel(
         nx_sb = lists.tile([P, S // LIST_ROWS], U16, name="nx_sb")
         w_raw = [keep.tile([P, 2, N], F32, name=f"w_raw{h}") for h in range(2)]
         words = keep.tile([P, T], I32, name="words")
-        scales = keep.tile([P, T], U8, name="scales")
-        win_y = [keep.tile([P, 2 * S], F32, name=f"win_y{t}") for t in range(PACK)]
+        late = ctx.enter_context(tc.tile_pool(name="late", bufs=1))
+        scales = late.tile([P, T], U8, name="scales", offset=3 * 1024)
+        rw_pair = [late.tile([P, 2, S], F32, name=f"rw_pair{u}", offset=4096 * u) for u in range(2)]
+        win_y = [
+            w_raw[t][:].rearrange("p j c -> p (j c)") if t in EARLY else keep.tile([P, 2 * S], F32, name=f"win_y{t}")[:]
+            for t in range(PACK)
+        ]
 
-        nc.vector.memset(scales[:].bitcast(I32), 0)
+        nc.vector.memset(scales[:96, :].bitcast(I32), 0)
+        nc.vector.memset(scales[96 : P - BLOCKS, :].bitcast(I32), 0)
 
         w_rows = w1.rearrange("(p j) c -> p j c", j=PACK)
-        nc.sync.dma_start(w_raw[0][:], w_rows[:, 0:2, :])
+        nc.scalar.dma_start(scales[P - BLOCKS :, :].bitcast(I32), x_scales[0].bitcast(I32))
         nc.sync.dma_start(offs_sb[:], offs)
-        for r in range(SCALE_ROWS):
-            nc.sync.dma_start(scales[r:P:QUADRANT, :].bitcast(I32), x_scales[0, r:BLOCKS:SCALE_ROWS, :].bitcast(I32))
+        nc.sync.dma_start(w_raw[0][:], w_rows[:, 0:2, :])
         nc.sync.dma_start(w_raw[1][:], w_rows[:, 2:4, :])
         nc.sync.dma_start(words[:], x_words[0].rearrange("p n t -> p (n t)").bitcast(I32))
         nc.sync.dma_start(nx_sb[:], nx)
         rw_rows = rw.rearrange("(p t) c -> p t c", t=PACK)
-        rw_sb = [win_y[t][:, S:] if t in EARLY else keep.tile([P, S], F32, name=f"rw_sb{t}")[:] for t in range(PACK)]
-        for t in range(PACK):
-            nc.sync.dma_start(rw_sb[t], rw_rows[:, t, :])
+        rw_sb = [rw_pair[t // 2][:, t % 2, :] for t in range(PACK)]
 
         w_bf = keep.tile([P, N * PACK], BF16, name="w_bf", tag="operand", align_bytes=64)
         w_out = w_bf[:].rearrange("p (t m j) -> p m j t", t=PACK, j=PACK)
@@ -71,9 +74,17 @@ def tile_picked_gae8_none_po_kernel(
             nc.vector.tensor_copy(w_out[:, : P // 2, 2 * h : 2 * h + 2, :], w_in[h][:, : P // 2])
             nc.scalar.activation(w_out[:, P // 2 :, 2 * h : 2 * h + 2, :], w_in[h][:, P // 2 :], COPY)
 
-        round_weights(0)
         x_sc = keep.tile([P, S], U8, name="x_sc", align_bytes=64)
-        nc.vector.tensor_copy(x_sc[:], scales[:].indirect(offs_sb[:]))
+        nc.vector.memset(x_sc[:].bitcast(I32), 0)
+        picked = keep.tile([P, S], U8, name="picked", align_bytes=64)
+        nc.vector.tensor_copy(picked[:], scales[:].indirect(offs_sb[:]))
+        for r in range(SCALE_ROWS):
+            nc.sync.dma_start(
+                x_sc[r:P:QUADRANT, :].bitcast(I32), picked[P - BLOCKS + r : P : SCALE_ROWS, :].bitcast(I32)
+            )
+        for u in range(2):
+            nc.sync.dma_start(rw_pair[u][:], rw_rows[:, 2 * u : 2 * u + 2, :])
+        round_weights(0)
         round_weights(1)
 
         w_codes = keep.tile([P, N], U32, name="w_codes", align_bytes=64)
@@ -105,13 +116,30 @@ def tile_picked_gae8_none_po_kernel(
         win_d = [keep.tile([P, 2 * S], F32, name=f"win_d{t}") for t in range(PACK)]
         diff = [win_d[t][:, S:] for t in range(PACK)]
 
-        for h in range(2):
-            for t in EARLY:
-                cols = slice(h * HALF, (h + 1) * HALF)
-                y = psum.tile([P, HALF], F32, name=f"y{t}_{h}", tag=f"bank{t}_{h}")
-                product(y[:], t, cols)
-                nc.vector.tensor_tensor(diff[t][:, cols], rw_sb[t][:, cols], y[:], SUBTRACT)
-                nc.scalar.activation(win_y[t][:, cols], y[:], COPY, scale=GAMMA)
+        halves = [slice(0, HALF), slice(HALF, S)]
+
+        def half_product(t, h, bank):
+            y = psum.tile([P, HALF], F32, name=f"y{t}_{h}_{bank}", tag=bank)
+            product(y[:], t, halves[h])
+            return y
+
+        def difference(t, h, y):
+            nc.vector.tensor_tensor(diff[t][:, halves[h]], rw_sb[t][:, halves[h]], y[:], SUBTRACT)
+
+        def window(t, h, y):
+            nc.scalar.activation(win_y[t][:, halves[h]], y[:], COPY, scale=GAMMA)
+
+        y00 = half_product(0, 0, "bank0_0")
+        window(0, 0, y00)
+        y10 = half_product(1, 0, "bank1_0")
+        window(0, 1, half_product(0, 1, "bank_s"))
+        difference(1, 0, y10)
+        difference(0, 0, y00)
+        difference(0, 1, half_product(0, 1, "bank0_1"))
+        y11 = half_product(1, 1, "bank1_1")
+        difference(1, 1, y11)
+        window(1, 0, y10)
+        window(1, 1, y11)
 
         minus_y = {t: win_y[t][:, S:] for t in LATE}
         turned = {}
@@ -152,7 +180,7 @@ def tile_picked_gae8_none_po_kernel(
         def turn_back(t):
             turned_sb = keep.tile([P, S], F32, name=f"turned_sb{t}")
             nc.scalar.activation(turned_sb[:], turned[t][:], COPY)
-            back[t] = psum.tile([P, S], F32, name=f"back{t}")
+            back[t] = psum.tile([P, S], F32, name=f"back{t}", tag=("bank_s", "bank0_0")[t - 2])
             for b in range(S // P):
                 cols = slice(b * P, (b + 1) * P)
                 nc.tensor.transpose(back[t][:, cols], turned_sb[:, cols], ident[:])
@@ -166,7 +194,7 @@ def tile_picked_gae8_none_po_kernel(
             nc.vector.tensor_tensor(res[0][:, t, :], win_d2[t][:].indirect(nx_sb[:]), d[t], ADD)
 
         for t in EARLY:
-            nc.vector.tensor_tensor(d[t], win_y[t][:].indirect(nx_sb[:]), diff[t], ADD)
+            nc.vector.tensor_tensor(d[t], win_y[t].indirect(nx_sb[:]), diff[t], ADD)
         for t in EARLY:
             turn(t + 2)
             second_step(t)
@@ -178,7 +206,7 @@ def tile_picked_gae8_none_po_kernel(
         for t in LATE:
             nc.scalar.activation(win_y[t][:, :S], minus_y[t], COPY, scale=-GAMMA * DAMP * DAMP)
             nc.scalar.activation(diff[t], back[t][:], COPY, scale=DAMP * DAMP)
-            nc.vector.tensor_tensor(win_d[t][:, :S], win_y[t][:].indirect(nx_sb[:]), diff[t], ADD)
+            nc.vector.tensor_tensor(win_d[t][:, :S], win_y[t].indirect(nx_sb[:]), diff[t], ADD)
 
         spans = list(zip(EDGES[:-1], EDGES[1:]))
         groups = [slice(c0 // LINE, c1 // LINE) for c0, c1 in spans]

@@ -23,7 +23,6 @@ QUADRANT = 32
 SCALE_ROWS = 4
 BLOCKS = 16
 LIST_ROWS = 16
-LINE = 4
 HALF = S // 2
 GAMMA = 0.9
 DAMP = 0.75
@@ -67,12 +66,12 @@ def tile_picked_gae8_none_po_kernel(
         rw_sb = [rw_pair[t // 2][:, t % 2, :] for t in range(PACK)]
 
         w_bf = keep.tile([P, N * PACK], BF16, name="w_bf", tag="operand", align_bytes=64)
-        w_out = w_bf[:].rearrange("p (t m j) -> p m j t", t=PACK, j=PACK)
-        w_in = [w_raw[h][:].rearrange("p j (m t) -> p m j t", t=PACK) for h in range(2)]
+        w_out = w_bf[:].rearrange("p (t m j) -> p m t j", t=PACK, j=PACK)
+        w_in = [w_raw[h][:].rearrange("p j (m t) -> p m t j", t=PACK) for h in range(2)]
 
         def round_weights(h):
-            nc.vector.tensor_copy(w_out[:, : P // 2, 2 * h : 2 * h + 2, :], w_in[h][:, : P // 2])
-            nc.scalar.activation(w_out[:, P // 2 :, 2 * h : 2 * h + 2, :], w_in[h][:, P // 2 :], COPY)
+            nc.vector.tensor_copy(w_out[:, : P // 2, :, 2 * h : 2 * h + 2], w_in[h][:, : P // 2])
+            nc.scalar.activation(w_out[:, P // 2 :, :, 2 * h : 2 * h + 2], w_in[h][:, P // 2 :], COPY)
 
         x_sc = keep.tile([P, S], U8, name="x_sc", align_bytes=64)
         nc.vector.memset(x_sc[:].bitcast(I32), 0)
@@ -165,8 +164,8 @@ def tile_picked_gae8_none_po_kernel(
         out_words = out_1[0].rearrange("p n t -> p (n t)").bitcast(I32)
         res = [keep.tile([P, 2, S], F32, name=f"res{u}") for u in range(2)]
         res_bf = keep.tile([P, S * PACK], BF16, name="res_bf", align_bytes=64)
-        rounded = res_bf[:].rearrange("p (c i t) -> p c t i", i=LINE, t=PACK)
-        exact = [res[u][:].rearrange("p t (c i) -> p c t i", i=LINE) for u in range(2)]
+        rounded = res_bf[:].rearrange("p (c t) -> p c t", t=PACK)
+        exact = [res[u][:].rearrange("p t c -> p c t") for u in range(2)]
 
         d = [keep.tile([P, S], F32, name=f"d{t}")[:] for t in range(PACK)]
         win_d2 = [
@@ -209,9 +208,9 @@ def tile_picked_gae8_none_po_kernel(
             nc.vector.tensor_tensor(win_d[t][:, :S], win_y[t].indirect(nx_sb[:]), diff[t], ADD)
 
         spans = list(zip(EDGES[:-1], EDGES[1:]))
-        groups = [slice(c0 // LINE, c1 // LINE) for c0, c1 in spans]
+        groups = [slice(c0, c1) for c0, c1 in spans]
         for t in LATE:
-            nc.scalar.copy(rounded[:, groups[t - 2], 0:2, :], exact[0][:, groups[t - 2]])
+            nc.scalar.copy(rounded[:, groups[t - 2], 0:2], exact[0][:, groups[t - 2]])
             nc.scalar.activation(damped[t][:], win_d[t][:, :S], COPY, scale=1.0 / DAMP)
             nc.vector.tensor_tensor(win_d2[t][:], win_d[t][:].indirect(nx_sb[:]), damped[t][:], ADD)
 
@@ -220,7 +219,7 @@ def tile_picked_gae8_none_po_kernel(
         nc.scalar.activation(d_out[:, :, LAST_PIECE:], d_in[:, :, LAST_PIECE:], COPY, scale=1.0 / (DAMP * DAMP))
         nc.scalar.activation(d[2], win_d[2][:, :S], COPY, scale=1.0 / (DAMP * DAMP))
         nc.scalar.activation(d_out[:, :, :LAST_PIECE], d_in[:, :, :LAST_PIECE], COPY, scale=1.0 / (DAMP * DAMP))
-        nc.scalar.copy(rounded[:, groups[2], 0:2, :], exact[0][:, groups[2]])
+        nc.scalar.copy(rounded[:, groups[2], 0:2], exact[0][:, groups[2]])
 
         for (c0, c1), group in zip(spans, groups):
             for t in LATE:
@@ -232,7 +231,7 @@ def tile_picked_gae8_none_po_kernel(
                 )
             if c1 % HALF == 0:
                 nc.sync.dma_start(out_rows[:, 2:4, c1 - HALF : c1], res[1][:, :, c1 - HALF : c1])
-            nc.scalar.copy(rounded[:, group, 2:4, :], exact[1][:, group])
+            nc.scalar.copy(rounded[:, group, 2:4], exact[1][:, group])
 
         o_codes = keep.tile([P, S], I32, name="o_codes", tag="last2", align_bytes=64)
         o_sc = keep.tile([P, S], U8, name="o_sc", align_bytes=64)

@@ -1,7 +1,6 @@
 from contextlib import ExitStack
 
 import concourse.mybir as mybir
-from concourse.masks import make_identity
 
 K, T, S, N = 512, 2048, 512, 512
 FLOPS = 2 * K * N * S
@@ -16,6 +15,7 @@ FP8X4 = mybir.dt.float8_e4m3fn_x4
 COPY = mybir.ActivationFunctionType.Copy
 ADD = mybir.AluOpType.add
 SUBTRACT = mybir.AluOpType.subtract
+MULT = mybir.AluOpType.mult
 
 P = 128
 PACK = 4
@@ -27,8 +27,7 @@ HALF = S // 2
 GAMMA = 0.9
 DAMP = 0.75
 EARLY, LATE = (0, 1), (2, 3)
-LAST_PIECE = 32
-EDGES = (0, 256, 384, 512)
+RANGE = 128
 
 
 def tile_picked_gae8_none_po_kernel(
@@ -46,11 +45,11 @@ def tile_picked_gae8_none_po_kernel(
         words = keep.tile([P, T], I32, name="words")
         late = ctx.enter_context(tc.tile_pool(name="late", bufs=1))
         scales = late.tile([P, T], U8, name="scales", offset=3 * 1024)
-        rw_pair = [late.tile([P, 2, S], F32, name=f"rw_pair{u}", offset=4096 * u) for u in range(2)]
-        win_y = [
-            w_raw[t][:].rearrange("p j c -> p (j c)") if t in EARLY else keep.tile([P, 2 * S], F32, name=f"win_y{t}")[:]
-            for t in range(PACK)
-        ]
+        rw_early = late.tile([P, 2, S], F32, name="rw_early", offset=0)
+        win_y2 = late.tile([P, 3, S], F32, name="win_y2", offset=4096)
+        win_y3 = keep.tile([P, 2 * S], F32, name="win_y3")
+        win_y = [w_raw[t][:].rearrange("p j c -> p (j c)") for t in EARLY]
+        win_y = win_y + [win_y2[:].rearrange("p j c -> p (j c)"), win_y3[:]]
 
         nc.vector.memset(scales[:96, :].bitcast(I32), 0)
         nc.vector.memset(scales[96 : P - BLOCKS, :].bitcast(I32), 0)
@@ -63,6 +62,7 @@ def tile_picked_gae8_none_po_kernel(
         nc.sync.dma_start(words[:], x_words[0].rearrange("p n t -> p (n t)").bitcast(I32))
         nc.sync.dma_start(nx_sb[:], nx)
         rw_rows = rw.rearrange("(p t) c -> p t c", t=PACK)
+        rw_pair = [rw_early[:], win_y2[:, 1:, :]]
         rw_sb = [rw_pair[t // 2][:, t % 2, :] for t in range(PACK)]
 
         w_bf = keep.tile([P, N * PACK], BF16, name="w_bf", tag="operand", align_bytes=64)
@@ -82,7 +82,7 @@ def tile_picked_gae8_none_po_kernel(
                 x_sc[r:P:QUADRANT, :].bitcast(I32), picked[P - BLOCKS + r : P : SCALE_ROWS, :].bitcast(I32)
             )
         for u in range(2):
-            nc.sync.dma_start(rw_pair[u][:], rw_rows[:, 2 * u : 2 * u + 2, :])
+            nc.sync.dma_start(rw_pair[u], rw_rows[:, 2 * u : 2 * u + 2, :])
         round_weights(0)
         round_weights(1)
 
@@ -97,10 +97,6 @@ def tile_picked_gae8_none_po_kernel(
                 x_codes[:, h * HALF : (h + 1) * HALF], words[:].bitcast(U32).indirect(offs_sb[:, entries])
             )
 
-        ident = keep.tile([P, P], F32, name="ident")
-        nc.vector.memset(ident[:], 0.0)
-        make_identity(nc, ident[:], nomemset=True)
-
         def product(y, t, cols):
             nc.tensor.matmul_mx(
                 out=y,
@@ -113,129 +109,105 @@ def tile_picked_gae8_none_po_kernel(
             )
 
         win_d = [keep.tile([P, 2 * S], F32, name=f"win_d{t}") for t in range(PACK)]
+        d = [win_d[t][:, :S] for t in range(PACK)]
         diff = [win_d[t][:, S:] for t in range(PACK)]
-
         halves = [slice(0, HALF), slice(HALF, S)]
+        whole = slice(0, S)
 
-        def half_product(t, h, bank):
-            y = psum.tile([P, HALF], F32, name=f"y{t}_{h}_{bank}", tag=bank)
-            product(y[:], t, halves[h])
+        def made(t, cols, bank):
+            y = psum.tile([P, cols.stop - cols.start], F32, name=f"y{t}_{bank}", tag=bank)
+            product(y[:], t, cols)
             return y
 
-        def difference(t, h, y):
-            nc.vector.tensor_tensor(diff[t][:, halves[h]], rw_sb[t][:, halves[h]], y[:], SUBTRACT)
+        def difference(t, cols, y):
+            nc.vector.tensor_tensor(diff[t][:, cols], rw_sb[t][:, cols], y[:], SUBTRACT)
 
-        def window(t, h, y):
-            nc.scalar.activation(win_y[t][:, halves[h]], y[:], COPY, scale=GAMMA)
+        def window(t, cols, y):
+            nc.scalar.activation(win_y[t][:, cols], y[:], COPY, scale=GAMMA)
 
-        y00 = half_product(0, 0, "bank0_0")
-        window(0, 0, y00)
-        y10 = half_product(1, 0, "bank1_0")
-        window(0, 1, half_product(0, 1, "bank_s"))
-        difference(1, 0, y10)
-        difference(0, 0, y00)
-        difference(0, 1, half_product(0, 1, "bank0_1"))
-        y11 = half_product(1, 1, "bank1_1")
-        difference(1, 1, y11)
-        window(1, 0, y10)
-        window(1, 1, y11)
+        def gather_add(dst, win, entries, plain):
+            nc.vector.tensor_tensor(dst, win.indirect(entries), plain, ADD)
 
-        minus_y = {t: win_y[t][:, S:] for t in LATE}
-        turned = {}
+        def fetch(dst, win, factor):
+            nc.scalar.activation(dst, win.indirect(nx_sb[:]), COPY, scale=factor)
 
-        def turn(t):
-            y = psum.tile([P, S], F32, name=f"y{t}", tag=f"bank{t - 2}_1")
-            product(y[:], t, slice(0, S))
-            nc.scalar.activation(minus_y[t], y[:], COPY, scale=-1.0)
-            turned[t] = psum.tile([P, S], F32, name=f"turned{t}")
-            for n, term in enumerate((rw_sb[t], minus_y[t])):
-                for b in range(S // P):
-                    cols = slice(b * P, (b + 1) * P)
-                    nc.tensor.matmul(
-                        turned[t][:, cols],
-                        term[:, cols],
-                        ident[:],
-                        start=(n == 0 and b == 0),
-                        stop=(n == 1 and b == S // P - 1),
-                        is_transpose=True,
-                    )
+        y00 = made(0, halves[0], "bank0_0")
+        window(0, halves[0], y00)
+        y10 = made(1, halves[0], "bank1_0")
+        window(0, halves[1], made(0, halves[1], "bank_s"))
+        difference(1, halves[0], y10)
+        difference(0, halves[0], y00)
+        difference(0, halves[1], made(0, halves[1], "bank0_1"))
+        y11 = made(1, halves[1], "bank1_1")
+        difference(1, halves[1], y11)
+        window(1, halves[0], y10)
+        window(1, halves[1], y11)
+        y_late = {t: made(t, whole, f"bank{t}") for t in LATE}
+        for t in LATE:
+            window(t, whole, y_late[t])
 
         out_rows = out_0.rearrange("(p t) c -> p t c", t=PACK)
         out_words = out_1[0].rearrange("p n t -> p (n t)").bitcast(I32)
-        res = [keep.tile([P, 2, S], F32, name=f"res{u}") for u in range(2)]
+        res = keep.tile([P, PACK, S], F32, name="res")
         res_bf = keep.tile([P, S * PACK], BF16, name="res_bf", align_bytes=64)
         rounded = res_bf[:].rearrange("p (c t) -> p c t", t=PACK)
-        exact = [res[u][:].rearrange("p t c -> p c t") for u in range(2)]
+        exact = res[:].rearrange("p t c -> p c t")
 
-        d = [keep.tile([P, S], F32, name=f"d{t}")[:] for t in range(PACK)]
-        win_d2 = [
-            keep.tile([P, 2 * S if t in EARLY else S], F32, name=f"win_d2{t}", tag=f"last{t}", align_bytes=64)
-            for t in range(PACK)
+        next_d = [win_y3[:, S:]] + [keep.tile([P, S], F32, name=f"next_d{t}")[:] for t in (1, 2, 3)]
+        next_d2 = [keep.tile([P, S], F32, name=f"next_d2{t}")[:] for t in EARLY]
+        win_d2 = [win_y[t] for t in EARLY] + [
+            keep.tile([P, S], F32, name=f"win_d2{t}", tag=f"last{t}", align_bytes=64)[:] for t in LATE
         ]
-        d2 = [win_d2[t][:, S:] for t in EARLY]
-        damped = {t: keep.tile([P, S], F32, name=f"damped{t}") for t in LATE}
-        back = {}
 
-        def turn_back(t):
-            turned_sb = keep.tile([P, S], F32, name=f"turned_sb{t}")
-            nc.scalar.activation(turned_sb[:], turned[t][:], COPY)
-            back[t] = psum.tile([P, S], F32, name=f"back{t}", tag=("bank_s", "bank0_0")[t - 2])
-            for b in range(S // P):
-                cols = slice(b * P, (b + 1) * P)
-                nc.tensor.transpose(back[t][:, cols], turned_sb[:, cols], ident[:])
+        def first_step(t):
+            gather_add(d[t], win_y[t], nx_sb[:], diff[t])
 
-        def second_step(t):
-            nc.scalar.activation(win_d[t][:, :S], d[t], COPY, scale=DAMP)
-            nc.vector.tensor_tensor(d2[t], win_d[t][:].indirect(nx_sb[:]), d[t], ADD)
+        def second_fetch(t):
+            fetch(next_d[t], win_d[t][:], DAMP if t in EARLY else DAMP * DAMP)
 
-        def last_step(t):
-            nc.scalar.activation(win_d2[t][:, :S], d2[t], COPY, scale=DAMP)
-            nc.vector.tensor_tensor(res[0][:, t, :], win_d2[t][:].indirect(nx_sb[:]), d[t], ADD)
+        def second_sum(t):
+            if t in EARLY:
+                nc.vector.tensor_tensor(win_d2[t][:, :S], next_d[t], d[t], ADD)
+            else:
+                nc.vector.scalar_tensor_tensor(win_d2[t], d[t], DAMP, next_d[t], MULT, ADD)
 
-        for t in EARLY:
-            nc.vector.tensor_tensor(d[t], win_y[t].indirect(nx_sb[:]), diff[t], ADD)
-        for t in EARLY:
-            turn(t + 2)
-            second_step(t)
-        for t in EARLY:
-            turn_back(t + 2)
-            last_step(t)
-        nc.sync.dma_start(out_rows[:, 0:2, :], res[0][:])
+        def last_fetch(t):
+            fetch(next_d2[t], win_d2[t], DAMP)
 
-        for t in LATE:
-            nc.scalar.activation(win_y[t][:, :S], minus_y[t], COPY, scale=-GAMMA * DAMP * DAMP)
-            nc.scalar.activation(diff[t], back[t][:], COPY, scale=DAMP * DAMP)
-            nc.vector.tensor_tensor(win_d[t][:, :S], win_y[t].indirect(nx_sb[:]), diff[t], ADD)
+        def last_sum(t):
+            nc.vector.tensor_tensor(res[:, t, :], next_d2[t], d[t], ADD)
 
-        spans = list(zip(EDGES[:-1], EDGES[1:]))
-        groups = [slice(c0, c1) for c0, c1 in spans]
-        for t in LATE:
-            nc.scalar.copy(rounded[:, groups[t - 2], 0:2], exact[0][:, groups[t - 2]])
-            nc.scalar.activation(damped[t][:], win_d[t][:, :S], COPY, scale=1.0 / DAMP)
-            nc.vector.tensor_tensor(win_d2[t][:], win_d[t][:].indirect(nx_sb[:]), damped[t][:], ADD)
+        first_step(0)
+        first_step(1)
+        second_fetch(0)
+        second_fetch(1)
+        difference(2, whole, y_late[2])
+        second_sum(0)
+        last_fetch(0)
+        first_step(2)
+        second_fetch(2)
+        difference(3, whole, y_late[3])
+        second_sum(1)
+        last_fetch(1)
+        first_step(3)
+        second_fetch(3)
+        last_sum(0)
+        second_sum(2)
+        last_sum(1)
+        nc.sync.dma_start(out_rows[:, 0:2, :], res[:, 0:2, :])
+        second_sum(3)
 
-        d_out = d[3].rearrange("p (g c) -> p g c", c=P)
-        d_in = win_d[3][:, :S].rearrange("p (g c) -> p g c", c=P)
-        nc.scalar.activation(d_out[:, :, LAST_PIECE:], d_in[:, :, LAST_PIECE:], COPY, scale=1.0 / (DAMP * DAMP))
-        nc.scalar.activation(d[2], win_d[2][:, :S], COPY, scale=1.0 / (DAMP * DAMP))
-        nc.scalar.activation(d_out[:, :, :LAST_PIECE], d_in[:, :, :LAST_PIECE], COPY, scale=1.0 / (DAMP * DAMP))
-        nc.scalar.copy(rounded[:, groups[2], 0:2], exact[0][:, groups[2]])
-
-        for (c0, c1), group in zip(spans, groups):
+        for c0 in range(0, S, RANGE):
+            c1 = c0 + RANGE
             for t in LATE:
-                nc.vector.tensor_tensor(
-                    res[1][:, t - 2, c0:c1],
-                    win_d2[t][:].indirect(nx_sb[:, c0 // LIST_ROWS : c1 // LIST_ROWS]),
-                    d[t][:, c0:c1],
-                    ADD,
-                )
+                gather_add(res[:, t, c0:c1], win_d2[t], nx_sb[:, c0 // LIST_ROWS : c1 // LIST_ROWS], d[t][:, c0:c1])
             if c1 % HALF == 0:
-                nc.sync.dma_start(out_rows[:, 2:4, c1 - HALF : c1], res[1][:, :, c1 - HALF : c1])
-            nc.scalar.copy(rounded[:, group, 2:4], exact[1][:, group])
+                nc.sync.dma_start(out_rows[:, 2:4, c1 - HALF : c1], res[:, 2:4, c1 - HALF : c1])
+            nc.scalar.copy(rounded[:, c0:c1], exact[:, c0:c1])
 
         o_codes = keep.tile([P, S], I32, name="o_codes", tag="last2", align_bytes=64)
         o_sc = keep.tile([P, S], U8, name="o_sc", align_bytes=64)
-        for c0, c1 in spans:
+        for c0, c1 in ((0, 256), (256, 384), (384, 512)):
             nc.vector.quantize_mx(
                 out=o_codes[:, c0:c1].bitcast(FP8X4), scales=o_sc[:, c0:c1], in_=res_bf[:, PACK * c0 : PACK * c1]
             )

@@ -27,7 +27,7 @@ HALF = S // 2
 GAMMA = 0.9
 DAMP = 0.75
 EARLY, LATE = (0, 1), (2, 3)
-RANGE = 128
+EDGES = (0, 256, 384, 512)
 
 
 def tile_picked_gae8_none_po_kernel(
@@ -131,83 +131,68 @@ def tile_picked_gae8_none_po_kernel(
         def fetch(dst, win, factor):
             nc.scalar.activation(dst, win.indirect(nx_sb[:]), COPY, scale=factor)
 
-        y00 = made(0, halves[0], "bank0_0")
-        window(0, halves[0], y00)
-        y10 = made(1, halves[0], "bank1_0")
-        window(0, halves[1], made(0, halves[1], "bank_s"))
-        difference(1, halves[0], y10)
-        difference(0, halves[0], y00)
-        difference(0, halves[1], made(0, halves[1], "bank0_1"))
-        y11 = made(1, halves[1], "bank1_1")
-        difference(1, halves[1], y11)
-        window(1, halves[0], y10)
-        window(1, halves[1], y11)
-        y_late = {t: made(t, whole, f"bank{t}") for t in LATE}
-        for t in LATE:
-            window(t, whole, y_late[t])
-
         out_rows = out_0.rearrange("(p t) c -> p t c", t=PACK)
         out_words = out_1[0].rearrange("p n t -> p (n t)").bitcast(I32)
         res = keep.tile([P, PACK, S], F32, name="res")
         res_bf = keep.tile([P, S * PACK], BF16, name="res_bf", align_bytes=64)
-        rounded = res_bf[:].rearrange("p (c t) -> p c t", t=PACK)
-        exact = res[:].rearrange("p t c -> p c t")
+        rounded = res_bf[:].rearrange("p (c i t) -> p c t i", t=PACK, i=PACK)
+        exact = res[:].rearrange("p t (c i) -> p c t i", i=PACK)
 
-        next_d = [win_y3[:, S:]] + [keep.tile([P, S], F32, name=f"next_d{t}")[:] for t in (1, 2, 3)]
-        next_d2 = [keep.tile([P, S], F32, name=f"next_d2{t}")[:] for t in EARLY]
-        win_d2 = [win_y[t] for t in EARLY] + [
-            keep.tile([P, S], F32, name=f"win_d2{t}", tag=f"last{t}", align_bytes=64)[:] for t in LATE
+        next_y2 = win_y3[:, S:]
+        next_d = [keep.tile([P, S], F32, name=f"next_d{t}")[:] for t in range(PACK)]
+        win_d2 = [win_y[0]] + [
+            keep.tile([P, S], F32, name=f"win_d2{t}", tag=f"last{t}", align_bytes=64)[:] for t in (1, 2, 3)
         ]
 
         def first_step(t):
             gather_add(d[t], win_y[t], nx_sb[:], diff[t])
 
         def second_fetch(t):
-            fetch(next_d[t], win_d[t][:], DAMP if t in EARLY else DAMP * DAMP)
+            fetch(next_d[t], win_d[t][:], DAMP * DAMP)
 
         def second_sum(t):
-            if t in EARLY:
-                nc.vector.tensor_tensor(win_d2[t][:, :S], next_d[t], d[t], ADD)
-            else:
-                nc.vector.scalar_tensor_tensor(win_d2[t], d[t], DAMP, next_d[t], MULT, ADD)
+            nc.vector.scalar_tensor_tensor(win_d2[t][:, :S], d[t], DAMP, next_d[t], MULT, ADD)
 
-        def last_fetch(t):
-            fetch(next_d2[t], win_d2[t], DAMP)
-
-        def last_sum(t):
-            nc.vector.tensor_tensor(res[:, t, :], next_d2[t], d[t], ADD)
-
+        for h in range(2):
+            for t in EARLY:
+                y = made(t, halves[h], f"bank{t}_{h}")
+                window(t, halves[h], y)
+                difference(t, halves[h], y)
+        y2 = made(2, whole, "bank2")
+        y3 = made(3, whole, "bank3")
+        window(2, whole, y2)
+        fetch(next_y2, win_y[2], 1.0)
         first_step(0)
         first_step(1)
+        window(3, whole, y3)
         second_fetch(0)
         second_fetch(1)
-        difference(2, whole, y_late[2])
-        second_sum(0)
-        last_fetch(0)
-        first_step(2)
+        difference(2, whole, y2)
+        nc.vector.tensor_tensor(d[2], next_y2, diff[2], ADD)
         second_fetch(2)
-        difference(3, whole, y_late[3])
-        second_sum(1)
-        last_fetch(1)
+        difference(3, whole, y3)
+        second_sum(0)
         first_step(3)
         second_fetch(3)
-        last_sum(0)
+        gather_add(res[:, 0, :], win_d2[0], nx_sb[:], d[0])
+        nc.sync.dma_start(out_rows[:, 0, :], res[:, 0, :])
+        second_sum(1)
         second_sum(2)
-        last_sum(1)
-        nc.sync.dma_start(out_rows[:, 0:2, :], res[:, 0:2, :])
-        second_sum(3)
 
-        for c0 in range(0, S, RANGE):
-            c1 = c0 + RANGE
-            for t in LATE:
+        spans = list(zip(EDGES[:-1], EDGES[1:]))
+        for c0, c1 in spans:
+            for t in (1, 2, 3):
+                if t == 3 and c0 == 0:
+                    second_sum(3)
+            for t in (1, 2, 3):
                 gather_add(res[:, t, c0:c1], win_d2[t], nx_sb[:, c0 // LIST_ROWS : c1 // LIST_ROWS], d[t][:, c0:c1])
             if c1 % HALF == 0:
-                nc.sync.dma_start(out_rows[:, 2:4, c1 - HALF : c1], res[:, 2:4, c1 - HALF : c1])
-            nc.scalar.copy(rounded[:, c0:c1], exact[:, c0:c1])
+                nc.sync.dma_start(out_rows[:, 1:4, c1 - HALF : c1], res[:, 1:4, c1 - HALF : c1])
+            nc.scalar.copy(rounded[:, c0 // PACK : c1 // PACK], exact[:, c0 // PACK : c1 // PACK])
 
         o_codes = keep.tile([P, S], I32, name="o_codes", tag="last2", align_bytes=64)
         o_sc = keep.tile([P, S], U8, name="o_sc", align_bytes=64)
-        for c0, c1 in ((0, 256), (256, 384), (384, 512)):
+        for c0, c1 in spans:
             nc.vector.quantize_mx(
                 out=o_codes[:, c0:c1].bitcast(FP8X4), scales=o_sc[:, c0:c1], in_=res_bf[:, PACK * c0 : PACK * c1]
             )

@@ -1,6 +1,7 @@
 from contextlib import ExitStack
 
 import concourse.mybir as mybir
+from concourse.masks import make_identity
 
 K, T, S, N = 512, 2048, 512, 512
 FLOPS = 2 * K * N * S
@@ -27,7 +28,7 @@ HALF = S // 2
 GAMMA = 0.9
 DAMP = 0.75
 EARLY, LATE = (0, 1), (2, 3)
-EDGES = (0, 256, 384, 512)
+EDGES = (0, 192, 384, 512)
 
 
 def tile_picked_gae8_none_po_kernel(
@@ -97,6 +98,11 @@ def tile_picked_gae8_none_po_kernel(
                 x_codes[:, h * HALF : (h + 1) * HALF], words[:].bitcast(U32).indirect(offs_sb[:, entries])
             )
 
+        nc.gpsimd.memset(win_y3[:, S:], 0.0)
+        ident = keep.tile([P, P], F32, name="ident")
+        nc.vector.memset(ident[:], 0.0)
+        make_identity(nc, ident[:], nomemset=True)
+
         def product(y, t, cols):
             nc.tensor.matmul_mx(
                 out=y,
@@ -135,14 +141,17 @@ def tile_picked_gae8_none_po_kernel(
         out_words = out_1[0].rearrange("p n t -> p (n t)").bitcast(I32)
         res = keep.tile([P, PACK, S], F32, name="res")
         res_bf = keep.tile([P, S * PACK], BF16, name="res_bf", align_bytes=64)
-        rounded = res_bf[:].rearrange("p (c i t) -> p c t i", t=PACK, i=PACK)
-        exact = res[:].rearrange("p t (c i) -> p c t i", i=PACK)
 
-        next_y2 = win_y3[:, S:]
-        next_d = [keep.tile([P, S], F32, name=f"next_d{t}")[:] for t in range(PACK)]
-        win_d2 = [win_y[0]] + [
-            keep.tile([P, S], F32, name=f"win_d2{t}", tag=f"last{t}", align_bytes=64)[:] for t in (1, 2, 3)
+        pairs_out = res_bf[:].rearrange("p (c t) -> p c t", t=PACK)
+        pairs_in = res[:].rearrange("p t c -> p c t")
+        next_y2 = diff[2]
+        turned_sb = keep.tile([P, S], F32, name="turned_sb")[:]
+        next_d = [keep.tile([P, S], F32, name=f"next_d{t}")[:] for t in (0, 1)]
+        next_d = next_d + [diff[3], keep.tile([P, S], F32, name="next_d3")[:]]
+        win_d2 = [win_y[t] for t in EARLY] + [
+            keep.tile([P, S], F32, name=f"win_d2{t}", tag=f"last{t}", align_bytes=64)[:] for t in LATE
         ]
+        blocks = [slice(b * P, (b + 1) * P) for b in range(S // P)]
 
         def first_step(t):
             gather_add(d[t], win_y[t], nx_sb[:], diff[t])
@@ -153,6 +162,9 @@ def tile_picked_gae8_none_po_kernel(
         def second_sum(t):
             nc.vector.scalar_tensor_tensor(win_d2[t][:, :S], d[t], DAMP, next_d[t], MULT, ADD)
 
+        def last_step(t, c0, c1):
+            gather_add(res[:, t, c0:c1], win_d2[t], nx_sb[:, c0 // LIST_ROWS : c1 // LIST_ROWS], d[t][:, c0:c1])
+
         for h in range(2):
             for t in EARLY:
                 y = made(t, halves[h], f"bank{t}_{h}")
@@ -160,42 +172,60 @@ def tile_picked_gae8_none_po_kernel(
                 difference(t, halves[h], y)
         y2 = made(2, whole, "bank2")
         y3 = made(3, whole, "bank3")
-        window(2, whole, y2)
-        fetch(next_y2, win_y[2], 1.0)
-        first_step(0)
-        first_step(1)
+        minus_y2 = win_y[2][:, :S]
+        nc.scalar.activation(minus_y2, y2[:], COPY, scale=-1.0)
         window(3, whole, y3)
+        fetch(next_y2, win_y[2], -GAMMA)
+        turned = psum.tile([P, S], F32, name="turned")
+        terms = (rw_sb[2], minus_y2, next_y2)
+        for n, term in enumerate(terms):
+            for b, cols in enumerate(blocks):
+                nc.tensor.matmul(
+                    turned[:, cols],
+                    term[:, cols],
+                    ident[:],
+                    start=(n == 0 and b == 0),
+                    stop=(n == len(terms) - 1 and b == len(blocks) - 1),
+                    is_transpose=True,
+                )
+        first_step(0)
+        difference(3, whole, y3)
+        first_step(1)
         second_fetch(0)
         second_fetch(1)
-        difference(2, whole, y2)
-        nc.vector.tensor_tensor(d[2], next_y2, diff[2], ADD)
-        second_fetch(2)
-        difference(3, whole, y3)
-        second_sum(0)
+        nc.scalar.activation(turned_sb, turned[:], COPY)
+        back = psum.tile([P, S], F32, name="back")
+        for cols in blocks:
+            nc.tensor.transpose(back[:, cols], turned_sb[:, cols], ident[:])
         first_step(3)
         second_fetch(3)
-        gather_add(res[:, 0, :], win_d2[0], nx_sb[:], d[0])
-        nc.sync.dma_start(out_rows[:, 0, :], res[:, 0, :])
+        nc.scalar.activation(d[2], back[:], COPY)
+        second_fetch(2)
+        second_sum(0)
         second_sum(1)
+        last_step(0, 0, S)
+        second_sum(3)
+        last_step(1, 0, S)
+        nc.sync.dma_start(out_rows[:, 0:2, :], res[:, 0:2, :])
         second_sum(2)
-
         spans = list(zip(EDGES[:-1], EDGES[1:]))
+        nc.scalar.copy(pairs_out[:, :, 0:2], pairs_in[:, :, 0:2])
+
         for c0, c1 in spans:
-            for t in (1, 2, 3):
-                if t == 3 and c0 == 0:
-                    second_sum(3)
-            for t in (1, 2, 3):
-                gather_add(res[:, t, c0:c1], win_d2[t], nx_sb[:, c0 // LIST_ROWS : c1 // LIST_ROWS], d[t][:, c0:c1])
-            if c1 % HALF == 0:
-                nc.sync.dma_start(out_rows[:, 1:4, c1 - HALF : c1], res[:, 1:4, c1 - HALF : c1])
-            nc.scalar.copy(rounded[:, c0 // PACK : c1 // PACK], exact[:, c0 // PACK : c1 // PACK])
+            for t in (3, 2):
+                last_step(t, c0, c1)
+            nc.sync.dma_start(out_rows[:, 2:4, c0:c1], res[:, 2:4, c0:c1])
+            if c1 < S:
+                nc.scalar.copy(pairs_out[:, c0:c1, 2:4], pairs_in[:, c0:c1, 2:4])
 
         o_codes = keep.tile([P, S], I32, name="o_codes", tag="last2", align_bytes=64)
         o_sc = keep.tile([P, S], U8, name="o_sc", align_bytes=64)
-        for c0, c1 in spans:
+        for c0, c1 in ((0, 256), (256, 384), (384, 512)):
             nc.vector.quantize_mx(
                 out=o_codes[:, c0:c1].bitcast(FP8X4), scales=o_sc[:, c0:c1], in_=res_bf[:, PACK * c0 : PACK * c1]
             )
+            if c0 == 0:
+                nc.vector.tensor_copy(pairs_out[:, EDGES[-2] :, 2:4], pairs_in[:, EDGES[-2] :, 2:4])
             if c1 % HALF == 0:
                 nc.sync.dma_start(out_words[:, c1 - HALF : c1], o_codes[:, c1 - HALF : c1])
 

@@ -28,7 +28,7 @@ HALF = S // 2
 GAMMA = 0.9
 DAMP = 0.75
 EARLY, LATE = (0, 1), (2, 3)
-EDGES = (0, 192, 384, 512)
+EDGES = (0, 160, 352, 512)
 
 
 def tile_picked_gae8_none_po_kernel(
@@ -141,9 +141,9 @@ def tile_picked_gae8_none_po_kernel(
         out_words = out_1[0].rearrange("p n t -> p (n t)").bitcast(I32)
         res = keep.tile([P, PACK, S], F32, name="res")
         res_bf = keep.tile([P, S * PACK], BF16, name="res_bf", align_bytes=64)
+        rounded = res_bf[:].rearrange("p (c i t) -> p c t i", t=PACK, i=PACK)
+        exact = res[:].rearrange("p t (c i) -> p c t i", i=PACK)
 
-        pairs_out = res_bf[:].rearrange("p (c t) -> p c t", t=PACK)
-        pairs_in = res[:].rearrange("p t c -> p c t")
         next_y2 = diff[2]
         turned_sb = keep.tile([P, S], F32, name="turned_sb")[:]
         next_d = [keep.tile([P, S], F32, name=f"next_d{t}")[:] for t in (0, 1)]
@@ -209,25 +209,24 @@ def tile_picked_gae8_none_po_kernel(
         nc.sync.dma_start(out_rows[:, 0:2, :], res[:, 0:2, :])
         second_sum(2)
         spans = list(zip(EDGES[:-1], EDGES[1:]))
-        nc.scalar.copy(pairs_out[:, :, 0:2], pairs_in[:, :, 0:2])
 
         for c0, c1 in spans:
             for t in (3, 2):
                 last_step(t, c0, c1)
             nc.sync.dma_start(out_rows[:, 2:4, c0:c1], res[:, 2:4, c0:c1])
             if c1 < S:
-                nc.scalar.copy(pairs_out[:, c0:c1, 2:4], pairs_in[:, c0:c1, 2:4])
+                nc.scalar.copy(rounded[:, c0 // PACK : c1 // PACK], exact[:, c0 // PACK : c1 // PACK])
 
         o_codes = keep.tile([P, S], I32, name="o_codes", tag="last2", align_bytes=64)
         o_sc = keep.tile([P, S], U8, name="o_sc", align_bytes=64)
-        for c0, c1 in ((0, 256), (256, 384), (384, 512)):
+        for c0, c1 in ((0, 128), (128, 384), (384, 512)):
             nc.vector.quantize_mx(
                 out=o_codes[:, c0:c1].bitcast(FP8X4), scales=o_sc[:, c0:c1], in_=res_bf[:, PACK * c0 : PACK * c1]
             )
             if c0 == 0:
-                nc.vector.tensor_copy(pairs_out[:, EDGES[-2] :, 2:4], pairs_in[:, EDGES[-2] :, 2:4])
-            if c1 % HALF == 0:
-                nc.sync.dma_start(out_words[:, c1 - HALF : c1], o_codes[:, c1 - HALF : c1])
+                nc.vector.tensor_copy(rounded[:, EDGES[-2] // PACK :], exact[:, EDGES[-2] // PACK :])
+            else:
+                nc.sync.dma_start(out_words[:, c0 // 384 * 384 : c1], o_codes[:, c0 // 384 * 384 : c1])
 
         for r in range(SCALE_ROWS):
             queue = nc.scalar if r % 2 == 0 else nc.sync

@@ -25,6 +25,7 @@ SCALE_ROWS = 4
 BLOCKS = 16
 LIST_ROWS = 16
 HALF = S // 2
+PAIR = 2
 GAMMA = 0.9
 DAMP = 0.75
 EARLY, LATE = (0, 1), (2, 3)
@@ -141,8 +142,8 @@ def tile_picked_gae8_none_po_kernel(
         out_words = out_1[0].rearrange("p n t -> p (n t)").bitcast(I32)
         res = keep.tile([P, PACK, S], F32, name="res")
         res_bf = keep.tile([P, S * PACK], BF16, name="res_bf", align_bytes=64)
-        rounded = res_bf[:].rearrange("p (c i t) -> p c t i", t=PACK, i=PACK)
-        exact = res[:].rearrange("p t (c i) -> p c t i", i=PACK)
+        rounded = res_bf[:].rearrange("p (c i t) -> p c t i", t=PACK, i=PAIR)
+        exact = res[:].rearrange("p t (c i) -> p c t i", i=PAIR)
 
         next_y2 = diff[2]
         turned_sb = keep.tile([P, S], F32, name="turned_sb")[:]
@@ -215,7 +216,7 @@ def tile_picked_gae8_none_po_kernel(
                 last_step(t, c0, c1)
             nc.sync.dma_start(out_rows[:, 2:4, c0:c1], res[:, 2:4, c0:c1])
             if c1 < S:
-                nc.scalar.copy(rounded[:, c0 // PACK : c1 // PACK], exact[:, c0 // PACK : c1 // PACK])
+                nc.scalar.copy(rounded[:, c0 // PAIR : c1 // PAIR], exact[:, c0 // PAIR : c1 // PAIR])
 
         o_codes = keep.tile([P, S], I32, name="o_codes", tag="last2", align_bytes=64)
         o_sc = keep.tile([P, S], U8, name="o_sc", align_bytes=64)
@@ -224,7 +225,7 @@ def tile_picked_gae8_none_po_kernel(
                 out=o_codes[:, c0:c1].bitcast(FP8X4), scales=o_sc[:, c0:c1], in_=res_bf[:, PACK * c0 : PACK * c1]
             )
             if c0 == 0:
-                nc.vector.tensor_copy(rounded[:, EDGES[-2] // PACK :], exact[:, EDGES[-2] // PACK :])
+                nc.vector.tensor_copy(rounded[:, EDGES[-2] // PAIR :], exact[:, EDGES[-2] // PAIR :])
             else:
                 nc.sync.dma_start(out_words[:, c0 // 384 * 384 : c1], o_codes[:, c0 // 384 * 384 : c1])
 

@@ -29,7 +29,7 @@ PAIR = 2
 GAMMA = 0.9
 DAMP = 0.75
 EARLY, LATE = (0, 1), (2, 3)
-EDGES = (0, 160, 352, 512)
+EDGES = (0, 160, 320, 512)
 
 
 def tile_picked_gae8_none_po_kernel(
@@ -148,10 +148,9 @@ def tile_picked_gae8_none_po_kernel(
         next_y2 = diff[2]
         turned_sb = keep.tile([P, S], F32, name="turned_sb")[:]
         next_d = [keep.tile([P, S], F32, name=f"next_d{t}")[:] for t in (0, 1)]
-        next_d = next_d + [diff[3], keep.tile([P, S], F32, name="next_d3")[:]]
-        win_d2 = [win_y[t] for t in EARLY] + [
-            keep.tile([P, S], F32, name=f"win_d2{t}", tag=f"last{t}", align_bytes=64)[:] for t in LATE
-        ]
+        next_d = next_d + [keep.tile([P, S], F32, name=f"next_d{t}")[:] for t in LATE]
+        win_d2 = [win_y[0], win_y[1], keep.tile([P, S], F32, name="win_d22", tag="last2", align_bytes=64)[:], win_y[3]]
+        next_d2 = next_y2[:, :HALF]
         blocks = [slice(b * P, (b + 1) * P) for b in range(S // P)]
 
         def first_step(t):
@@ -204,30 +203,33 @@ def tile_picked_gae8_none_po_kernel(
         second_fetch(2)
         second_sum(0)
         second_sum(1)
-        last_step(0, 0, S)
+        last_step(0, HALF, S)
+        last_step(1, 0, HALF)
         second_sum(3)
-        last_step(1, 0, S)
-        nc.sync.dma_start(out_rows[:, 0:2, :], res[:, 0:2, :])
+        last_step(1, HALF, S)
+        nc.sync.dma_start(out_rows[:, 1, :], res[:, 1, :])
+        last_step(3, 0, S)
+        nc.sync.dma_start(out_rows[:, 3, :], res[:, 3, :])
+        nc.scalar.activation(next_d2, win_d2[0].indirect(nx_sb[:, : HALF // LIST_ROWS]), COPY)
         second_sum(2)
+        nc.vector.tensor_tensor(res[:, 0, :HALF], next_d2, d[0][:, :HALF], ADD)
+        nc.sync.dma_start(out_rows[:, 0, :], res[:, 0, :])
         spans = list(zip(EDGES[:-1], EDGES[1:]))
-
         for c0, c1 in spans:
-            for t in (3, 2):
-                last_step(t, c0, c1)
-            nc.sync.dma_start(out_rows[:, 2:4, c0:c1], res[:, 2:4, c0:c1])
+            last_step(2, c0, c1)
             if c1 < S:
                 nc.scalar.copy(rounded[:, c0 // PAIR : c1 // PAIR], exact[:, c0 // PAIR : c1 // PAIR])
+        nc.sync.dma_start(out_rows[:, 2, :], res[:, 2, :])
 
         o_codes = keep.tile([P, S], I32, name="o_codes", tag="last2", align_bytes=64)
         o_sc = keep.tile([P, S], U8, name="o_sc", align_bytes=64)
-        for c0, c1 in ((0, 128), (128, 384), (384, 512)):
+        for c0, c1 in ((0, 128), (384, 512), (128, 384)):
             nc.vector.quantize_mx(
                 out=o_codes[:, c0:c1].bitcast(FP8X4), scales=o_sc[:, c0:c1], in_=res_bf[:, PACK * c0 : PACK * c1]
             )
             if c0 == 0:
                 nc.vector.tensor_copy(rounded[:, EDGES[-2] // PAIR :], exact[:, EDGES[-2] // PAIR :])
-            else:
-                nc.sync.dma_start(out_words[:, c0 // 384 * 384 : c1], o_codes[:, c0 // 384 * 384 : c1])
+            nc.sync.dma_start(out_words[:, c0:c1], o_codes[:, c0:c1])
 
         for r in range(SCALE_ROWS):
             queue = nc.scalar if r % 2 == 0 else nc.sync

@@ -68,12 +68,12 @@ def tile_picked_gae8_none_po_kernel(
         rw_sb = [rw_pair[t // 2][:, t % 2, :] for t in range(PACK)]
 
         w_bf = keep.tile([P, N * PACK], BF16, name="w_bf", tag="operand", align_bytes=64)
-        w_out = w_bf[:].rearrange("p (t m j) -> p m t j", t=PACK, j=PACK)
-        w_in = [w_raw[h][:].rearrange("p j (m t) -> p m t j", t=PACK) for h in range(2)]
+        w_out = w_bf[:].rearrange("p (t a i j) -> p a t i j", t=PACK, i=PAIR, j=PACK)
+        w_in = [w_raw[h][:].rearrange("p j (a i t) -> p a t i j", t=PACK, i=PAIR) for h in range(2)]
 
         def round_weights(h):
-            nc.vector.tensor_copy(w_out[:, : P // 2, :, 2 * h : 2 * h + 2], w_in[h][:, : P // 2])
-            nc.scalar.activation(w_out[:, P // 2 :, :, 2 * h : 2 * h + 2], w_in[h][:, P // 2 :], COPY)
+            nc.vector.tensor_copy(w_out[:, : P // 4, :, :, 2 * h : 2 * h + 2], w_in[h][:, : P // 4])
+            nc.scalar.copy(w_out[:, P // 4 :, :, :, 2 * h : 2 * h + 2], w_in[h][:, P // 4 :])
 
         x_sc = keep.tile([P, S], U8, name="x_sc", align_bytes=64)
         nc.vector.memset(x_sc[:].bitcast(I32), 0)

@@ -28,7 +28,9 @@ HALF = S // 2
 PAIR = 2
 GAMMA = 0.9
 DAMP = 0.75
-EARLY, LATE = (0, 1), (2, 3)
+EARLY = (0, 1)
+WINDOW = 2 * S * 4
+APART = 32 * 1024
 EDGES = (0, 160, 320, 512)
 
 
@@ -43,13 +45,14 @@ def tile_picked_gae8_none_po_kernel(
 
         offs_sb = lists.tile([P, S // LIST_ROWS], U16, name="offs_sb")
         nx_sb = lists.tile([P, S // LIST_ROWS], U16, name="nx_sb")
-        w_raw = [keep.tile([P, 2, N], F32, name=f"w_raw{h}") for h in range(2)]
+        far = ctx.enter_context(tc.tile_pool(name="far", bufs=1))
+        w_raw = [far.tile([P, 2, N], F32, name=f"w_raw{h}", offset=5 * APART + h * WINDOW) for h in range(2)]
         words = keep.tile([P, T], I32, name="words")
         late = ctx.enter_context(tc.tile_pool(name="late", bufs=1))
         scales = late.tile([P, T], U8, name="scales", offset=3 * 1024)
         rw_early = late.tile([P, 2, S], F32, name="rw_early", offset=0)
         win_y2 = late.tile([P, 3, S], F32, name="win_y2", offset=4096)
-        win_y3 = keep.tile([P, 2 * S], F32, name="win_y3")
+        win_y3 = far.tile([P, 2 * S], F32, name="win_y3", offset=5 * APART + 2 * WINDOW)
         win_y = [w_raw[t][:].rearrange("p j c -> p (j c)") for t in EARLY]
         win_y = win_y + [win_y2[:].rearrange("p j c -> p (j c)"), win_y3[:]]
 
@@ -115,7 +118,7 @@ def tile_picked_gae8_none_po_kernel(
                 stop=True,
             )
 
-        win_d = [keep.tile([P, 2 * S], F32, name=f"win_d{t}") for t in range(PACK)]
+        win_d = [far.tile([P, 2 * S], F32, name=f"win_d{t}", offset=t * APART) for t in range(PACK)]
         d = [win_d[t][:, :S] for t in range(PACK)]
         diff = [win_d[t][:, S:] for t in range(PACK)]
         halves = [slice(0, HALF), slice(HALF, S)]
@@ -147,9 +150,9 @@ def tile_picked_gae8_none_po_kernel(
 
         next_y2 = diff[2]
         turned_sb = keep.tile([P, S], F32, name="turned_sb")[:]
-        next_d = [keep.tile([P, S], F32, name=f"next_d{t}")[:] for t in (0, 1)]
-        next_d = next_d + [keep.tile([P, S], F32, name=f"next_d{t}")[:] for t in LATE]
-        win_d2 = [win_y[0], win_y[1], keep.tile([P, S], F32, name="win_d22", tag="last2", align_bytes=64)[:], win_y[3]]
+        next_d = [far.tile([P, S], F32, name=f"next_d{t}", offset=4 * APART + t * WINDOW)[:] for t in range(PACK)]
+        win_d22 = far.tile([P, S], F32, name="win_d22", offset=5 * APART + 3 * WINDOW, align_bytes=64)
+        win_d2 = [win_y[0], win_y[1], win_d22[:], win_y[3]]
         next_d2 = next_y2[:, :HALF]
         blocks = [slice(b * P, (b + 1) * P) for b in range(S // P)]
 
@@ -221,7 +224,7 @@ def tile_picked_gae8_none_po_kernel(
                 nc.scalar.copy(rounded[:, c0 // PAIR : c1 // PAIR], exact[:, c0 // PAIR : c1 // PAIR])
         nc.sync.dma_start(out_rows[:, 2, :], res[:, 2, :])
 
-        o_codes = keep.tile([P, S], I32, name="o_codes", tag="last2", align_bytes=64)
+        o_codes = far.tile([P, S], I32, name="o_codes", offset=5 * APART + 3 * WINDOW, align_bytes=64)
         o_sc = keep.tile([P, S], U8, name="o_sc", align_bytes=64)
         for c0, c1 in ((0, 128), (384, 512), (128, 384)):
             nc.vector.quantize_mx(

@@ -32,6 +32,7 @@ EARLY = (0, 1)
 WINDOW = 2 * S * 4
 APART = 32 * 1024
 EDGES = (0, 160, 320, 512)
+VECTOR_SHARE = 80
 
 
 def tile_picked_gae8_none_po_kernel(
@@ -70,13 +71,14 @@ def tile_picked_gae8_none_po_kernel(
         rw_pair = [rw_early[:], win_y2[:, 1:, :]]
         rw_sb = [rw_pair[t // 2][:, t % 2, :] for t in range(PACK)]
 
-        w_bf = keep.tile([P, N * PACK], BF16, name="w_bf", tag="operand", align_bytes=64)
+        w_bf = keep.tile([P, N * PACK], BF16, name="w_bf", align_bytes=64)
         w_out = w_bf[:].rearrange("p (t a i j) -> p a t i j", t=PACK, i=PAIR, j=PACK)
         w_in = [w_raw[h][:].rearrange("p j (a i t) -> p a t i j", t=PACK, i=PAIR) for h in range(2)]
 
         def round_weights(h):
-            nc.vector.tensor_copy(w_out[:, : P // 4, :, :, 2 * h : 2 * h + 2], w_in[h][:, : P // 4])
-            nc.scalar.copy(w_out[:, P // 4 :, :, :, 2 * h : 2 * h + 2], w_in[h][:, P // 4 :])
+            cut = VECTOR_SHARE // PAIR
+            nc.vector.tensor_copy(w_out[:, :cut, :, :, 2 * h : 2 * h + 2], w_in[h][:, :cut])
+            nc.scalar.copy(w_out[:, cut:, :, :, 2 * h : 2 * h + 2], w_in[h][:, cut:])
 
         x_sc = keep.tile([P, S], U8, name="x_sc", align_bytes=64)
         nc.vector.memset(x_sc[:].bitcast(I32), 0)
@@ -95,7 +97,7 @@ def tile_picked_gae8_none_po_kernel(
         w_sc = keep.tile([P, N], U8, name="w_sc", align_bytes=64)
         nc.vector.quantize_mx(out=w_codes[:].bitcast(FP8X4), scales=w_sc[:], in_=w_bf[:])
 
-        x_codes = keep.tile([P, S], U32, name="x_codes", tag="operand", align_bytes=64)
+        x_codes = keep.tile([P, S], U32, name="x_codes", align_bytes=64)
         for h in range(2):
             entries = slice(h * HALF // LIST_ROWS, (h + 1) * HALF // LIST_ROWS)
             nc.vector.tensor_copy(

@@ -31,7 +31,7 @@ DAMP = 0.75
 EARLY = (0, 1)
 WINDOW = 2 * S * 4
 APART = 32 * 1024
-EDGES = (0, 160, 320, 512)
+EDGES = (0, 128, 320, 512)
 VECTOR_SHARE = 80
 
 
@@ -220,10 +220,12 @@ def tile_picked_gae8_none_po_kernel(
         nc.vector.tensor_tensor(res[:, 0, :HALF], next_d2, d[0][:, :HALF], ADD)
         nc.sync.dma_start(out_rows[:, 0, :], res[:, 0, :])
         spans = list(zip(EDGES[:-1], EDGES[1:]))
-        for c0, c1 in spans:
+        fetched = keep.tile([P, S - EDGES[2]], F32, name="fetched")[:]
+        nc.scalar.activation(fetched, win_d2[2].indirect(nx_sb[:, EDGES[2] // LIST_ROWS :]), COPY)
+        for c0, c1 in spans[:2]:
             last_step(2, c0, c1)
-            if c1 < S:
-                nc.scalar.copy(rounded[:, c0 // PAIR : c1 // PAIR], exact[:, c0 // PAIR : c1 // PAIR])
+            nc.scalar.copy(rounded[:, c0 // PAIR : c1 // PAIR], exact[:, c0 // PAIR : c1 // PAIR])
+        nc.vector.tensor_tensor(res[:, 2, EDGES[2] :], fetched, d[2][:, EDGES[2] :], ADD)
         nc.sync.dma_start(out_rows[:, 2, :], res[:, 2, :])
 
         o_codes = far.tile([P, S], I32, name="o_codes", offset=5 * APART + 3 * WINDOW, align_bytes=64)

@@ -173,7 +173,10 @@ def tile_picked_gae8_none_po_kernel(
         for h in range(2):
             for t in EARLY:
                 y = made(t, halves[h], f"bank{t}_{h}")
-                window(t, halves[h], y)
+                if (t, h) == (0, 0):
+                    nc.vector.tensor_scalar_mul(win_y[t][:, halves[h]], y[:], GAMMA)
+                else:
+                    window(t, halves[h], y)
                 difference(t, halves[h], y)
         y2 = made(2, whole, "bank2")
         y3 = made(3, whole, "bank3")

@@ -155,7 +155,7 @@ def tile_picked_gae8_none_po_kernel(
         next_d = [far.tile([P, S], F32, name=f"next_d{t}", offset=4 * APART + t * WINDOW)[:] for t in range(PACK)]
         win_d22 = far.tile([P, S], F32, name="win_d22", offset=5 * APART + 3 * WINDOW, align_bytes=64)
         win_d2 = [win_y[0], win_y[1], win_d22[:], win_y[3]]
-        next_d2 = next_y2[:, :HALF]
+        next_d2 = win_y[1][:, S : S + HALF]
         blocks = [slice(b * P, (b + 1) * P) for b in range(S // P)]
 
         def first_step(t):

from contextlib import ExitStack

import concourse.mybir as mybir
from concourse.masks import make_identity

K, T, S, N = 512, 2048, 512, 512
FLOPS = 2 * K * N * S

F32 = mybir.dt.float32
BF16 = mybir.dt.bfloat16
I32 = mybir.dt.int32
U32 = mybir.dt.uint32
U16 = mybir.dt.uint16
U8 = mybir.dt.uint8
FP8X4 = mybir.dt.float8_e4m3fn_x4
COPY = mybir.ActivationFunctionType.Copy
ADD = mybir.AluOpType.add
SUBTRACT = mybir.AluOpType.subtract
MULT = mybir.AluOpType.mult

P = 128
PACK = 4
QUADRANT = 32
SCALE_ROWS = 4
BLOCKS = 16
LIST_ROWS = 16
HALF = S // 2
PAIR = 2
GAMMA = 0.9
DAMP = 0.75
EARLY = (0, 1)
WINDOW = 2 * S * 4
APART = 32 * 1024
EDGES = (0, 128, 320, 512)
VECTOR_SHARE = 80


def tile_picked_gae8_none_po_kernel(
    tc, x_words, x_scales, w1, rw, offs, nx, out_0, out_1, out_2
):
    nc = tc.nc
    with ExitStack() as ctx:
        lists = ctx.enter_context(tc.tile_pool(name="lists", bufs=1))
        keep = ctx.enter_context(tc.tile_pool(name="keep", bufs=1))
        psum = ctx.enter_context(tc.psum_pool(name="psum", bufs=1))

        offs_sb = lists.tile([P, S // LIST_ROWS], U16, name="offs_sb")
        nx_sb = lists.tile([P, S // LIST_ROWS], U16, name="nx_sb")
        far = ctx.enter_context(tc.tile_pool(name="far", bufs=1))
        w_raw = [far.tile([P, 2, N], F32, name=f"w_raw{h}", offset=5 * APART + h * WINDOW) for h in range(2)]
        words = keep.tile([P, T], I32, name="words")
        late = ctx.enter_context(tc.tile_pool(name="late", bufs=1))
        scales = late.tile([P, T], U8, name="scales", offset=3 * 1024)
        rw_early = late.tile([P, 2, S], F32, name="rw_early", offset=0)
        win_y2 = late.tile([P, 3, S], F32, name="win_y2", offset=4096)
        win_y3 = far.tile([P, 2 * S], F32, name="win_y3", offset=5 * APART + 2 * WINDOW)
        win_y = [w_raw[t][:].rearrange("p j c -> p (j c)") for t in EARLY]
        win_y = win_y + [win_y2[:].rearrange("p j c -> p (j c)"), win_y3[:]]

        nc.vector.memset(scales[:96, :].bitcast(I32), 0)
        nc.vector.memset(scales[96 : P - BLOCKS, :].bitcast(I32), 0)

        w_rows = w1.rearrange("(p j) c -> p j c", j=PACK)
        nc.scalar.dma_start(scales[P - BLOCKS :, :].bitcast(I32), x_scales[0].bitcast(I32))
        nc.sync.dma_start(offs_sb[:], offs)
        nc.sync.dma_start(w_raw[0][:], w_rows[:, 0:2, :])
        nc.sync.dma_start(w_raw[1][:], w_rows[:, 2:4, :])
        nc.sync.dma_start(words[:], x_words[0].rearrange("p n t -> p (n t)").bitcast(I32))
        nc.sync.dma_start(nx_sb[:], nx)
        rw_rows = rw.rearrange("(p t) c -> p t c", t=PACK)
        rw_pair = [rw_early[:], win_y2[:, 1:, :]]
        rw_sb = [rw_pair[t // 2][:, t % 2, :] for t in range(PACK)]

        w_bf = keep.tile([P, N * PACK], BF16, name="w_bf", align_bytes=64)
        w_out = w_bf[:].rearrange("p (t a i j) -> p a t i j", t=PACK, i=PAIR, j=PACK)
        w_in = [w_raw[h][:].rearrange("p j (a i t) -> p a t i j", t=PACK, i=PAIR) for h in range(2)]

        def round_weights(h):
            cut = VECTOR_SHARE // PAIR
            nc.vector.tensor_copy(w_out[:, :cut, :, :, 2 * h : 2 * h + 2], w_in[h][:, :cut])
            nc.scalar.copy(w_out[:, cut:, :, :, 2 * h : 2 * h + 2], w_in[h][:, cut:])

        x_sc = keep.tile([P, S], U8, name="x_sc", align_bytes=64)
        nc.vector.memset(x_sc[:].bitcast(I32), 0)
        picked = keep.tile([P, S], U8, name="picked", align_bytes=64)
        nc.vector.tensor_copy(picked[:], scales[:].indirect(offs_sb[:]))
        for r in range(SCALE_ROWS):
            nc.sync.dma_start(
                x_sc[r:P:QUADRANT, :].bitcast(I32), picked[P - BLOCKS + r : P : SCALE_ROWS, :].bitcast(I32)
            )
        for u in range(2):
            nc.sync.dma_start(rw_pair[u], rw_rows[:, 2 * u : 2 * u + 2, :])
        round_weights(0)
        round_weights(1)

        w_codes = keep.tile([P, N], U32, name="w_codes", align_bytes=64)
        w_sc = keep.tile([P, N], U8, name="w_sc", align_bytes=64)
        nc.vector.quantize_mx(out=w_codes[:].bitcast(FP8X4), scales=w_sc[:], in_=w_bf[:])

        x_codes = keep.tile([P, S], U32, name="x_codes", align_bytes=64)
        for h in range(2):
            entries = slice(h * HALF // LIST_ROWS, (h + 1) * HALF // LIST_ROWS)
            nc.vector.tensor_copy(
                x_codes[:, h * HALF : (h + 1) * HALF], words[:].bitcast(U32).indirect(offs_sb[:, entries])
            )

        nc.gpsimd.memset(win_y3[:, S:], 0.0)
        ident = keep.tile([P, P], F32, name="ident")
        nc.vector.memset(ident[:], 0.0)
        make_identity(nc, ident[:], nomemset=True)

        def product(y, t, cols):
            nc.tensor.matmul_mx(
                out=y,
                lhsT=w_codes[:, t * P : (t + 1) * P].bitcast(FP8X4),
                lhsT_scale=w_sc[:, t * P : (t + 1) * P],
                rhs=x_codes[:, cols].bitcast(FP8X4),
                rhs_scale=x_sc[:, cols],
                start=True,
                stop=True,
            )

        win_d = [far.tile([P, 2 * S], F32, name=f"win_d{t}", offset=t * APART) for t in range(PACK)]
        d = [win_d[t][:, :S] for t in range(PACK)]
        diff = [win_d[t][:, S:] for t in range(PACK)]
        halves = [slice(0, HALF), slice(HALF, S)]
        whole = slice(0, S)

        def made(t, cols, bank):
            y = psum.tile([P, cols.stop - cols.start], F32, name=f"y{t}_{bank}", tag=bank)
            product(y[:], t, cols)
            return y

        def difference(t, cols, y):
            nc.vector.tensor_tensor(diff[t][:, cols], rw_sb[t][:, cols], y[:], SUBTRACT)

        def window(t, cols, y):
            nc.scalar.activation(win_y[t][:, cols], y[:], COPY, scale=GAMMA)

        def gather_add(dst, win, entries, plain):
            nc.vector.tensor_tensor(dst, win.indirect(entries), plain, ADD)

        def fetch(dst, win, factor):
            nc.scalar.activation(dst, win.indirect(nx_sb[:]), COPY, scale=factor)

        out_rows = out_0.rearrange("(p t) c -> p t c", t=PACK)
        out_words = out_1[0].rearrange("p n t -> p (n t)").bitcast(I32)
        res = keep.tile([P, PACK, S], F32, name="res")
        res_bf = keep.tile([P, S * PACK], BF16, name="res_bf", align_bytes=64)
        rounded = res_bf[:].rearrange("p (c i t) -> p c t i", t=PACK, i=PAIR)
        exact = res[:].rearrange("p t (c i) -> p c t i", i=PAIR)

        next_y2 = diff[2]
        turned_sb = keep.tile([P, S], F32, name="turned_sb")[:]
        next_d = [far.tile([P, S], F32, name=f"next_d{t}", offset=4 * APART + t * WINDOW)[:] for t in range(PACK)]
        win_d22 = far.tile([P, S], F32, name="win_d22", offset=5 * APART + 3 * WINDOW, align_bytes=64)
        win_d2 = [win_y[0], win_y[1], win_d22[:], win_y[3]]
        next_d2 = win_y[1][:, S : S + HALF]
        blocks = [slice(b * P, (b + 1) * P) for b in range(S // P)]

        def first_step(t):
            gather_add(d[t], win_y[t], nx_sb[:], diff[t])

        def second_fetch(t):
            fetch(next_d[t], win_d[t][:], DAMP * DAMP)

        def second_sum(t):
            nc.vector.scalar_tensor_tensor(win_d2[t][:, :S], d[t], DAMP, next_d[t], MULT, ADD)

        def last_step(t, c0, c1):
            gather_add(res[:, t, c0:c1], win_d2[t], nx_sb[:, c0 // LIST_ROWS : c1 // LIST_ROWS], d[t][:, c0:c1])

        for h in range(2):
            for t in EARLY:
                y = made(t, halves[h], f"bank{t}_{h}")
                if (t, h) == (0, 0):
                    nc.vector.tensor_scalar_mul(win_y[t][:, halves[h]], y[:], GAMMA)
                else:
                    window(t, halves[h], y)
                difference(t, halves[h], y)
        y2 = made(2, whole, "bank2")
        y3 = made(3, whole, "bank3")
        minus_y2 = win_y[2][:, :S]
        nc.scalar.activation(minus_y2, y2[:], COPY, scale=-1.0)
        window(3, whole, y3)
        fetch(next_y2, win_y[2], -GAMMA)
        turned = psum.tile([P, S], F32, name="turned")
        terms = (rw_sb[2], minus_y2, next_y2)
        for n, term in enumerate(terms):
            for b, cols in enumerate(blocks):
                nc.tensor.matmul(
                    turned[:, cols],
                    term[:, cols],
                    ident[:],
                    start=(n == 0 and b == 0),
                    stop=(n == len(terms) - 1 and b == len(blocks) - 1),
                    is_transpose=True,
                )
        first_step(0)
        difference(3, whole, y3)
        first_step(1)
        second_fetch(0)
        second_fetch(1)
        nc.scalar.activation(turned_sb, turned[:], COPY)
        back = psum.tile([P, S], F32, name="back")
        for cols in blocks:
            nc.tensor.transpose(back[:, cols], turned_sb[:, cols], ident[:])
        first_step(3)
        second_fetch(3)
        nc.scalar.activation(d[2], back[:], COPY)
        second_fetch(2)
        second_sum(0)
        second_sum(1)
        last_step(0, HALF, S)
        last_step(1, 0, HALF)
        second_sum(3)
        last_step(1, HALF, S)
        nc.sync.dma_start(out_rows[:, 1, :], res[:, 1, :])
        last_step(3, 0, S)
        nc.sync.dma_start(out_rows[:, 3, :], res[:, 3, :])
        nc.scalar.activation(next_d2, win_d2[0].indirect(nx_sb[:, : HALF // LIST_ROWS]), COPY)
        second_sum(2)
        nc.vector.tensor_tensor(res[:, 0, :HALF], next_d2, d[0][:, :HALF], ADD)
        nc.sync.dma_start(out_rows[:, 0, :], res[:, 0, :])
        spans = list(zip(EDGES[:-1], EDGES[1:]))
        fetched = keep.tile([P, S - EDGES[2]], F32, name="fetched")[:]
        nc.scalar.activation(fetched, win_d2[2].indirect(nx_sb[:, EDGES[2] // LIST_ROWS :]), COPY)
        for c0, c1 in spans[:2]:
            last_step(2, c0, c1)
            nc.scalar.copy(rounded[:, c0 // PAIR : c1 // PAIR], exact[:, c0 // PAIR : c1 // PAIR])
        nc.vector.tensor_tensor(res[:, 2, EDGES[2] :], fetched, d[2][:, EDGES[2] :], ADD)
        nc.sync.dma_start(out_rows[:, 2, :], res[:, 2, :])

        o_codes = far.tile([P, S], I32, name="o_codes", offset=5 * APART + 3 * WINDOW, align_bytes=64)
        o_sc = keep.tile([P, S], U8, name="o_sc", align_bytes=64)
        for c0, c1 in ((0, 128), (384, 512), (128, 384)):
            nc.vector.quantize_mx(
                out=o_codes[:, c0:c1].bitcast(FP8X4), scales=o_sc[:, c0:c1], in_=res_bf[:, PACK * c0 : PACK * c1]
            )
            if c0 == 0:
                nc.vector.tensor_copy(rounded[:, EDGES[-2] // PAIR :], exact[:, EDGES[-2] // PAIR :])
            nc.sync.dma_start(out_words[:, c0:c1], o_codes[:, c0:c1])

        for r in range(SCALE_ROWS):
            queue = nc.scalar if r % 2 == 0 else nc.sync
            queue.dma_start(out_2[0, r:BLOCKS:SCALE_ROWS, :].bitcast(I32), o_sc[r:P:QUADRANT, :].bitcast(I32))
